import numpy as np, ml_dtypes
CORES = [16,18,20,22]
N = 4
import mx_ref
BF = ml_dtypes.bfloat16
def cols(t, e):
    v = np.concatenate([t.reshape(128, -1, 4), np.zeros((128, 1, 4), BF)], axis=1)
    return np.ascontiguousarray(v[:, e]).reshape(128, -1)
def f(rng, *shape):
    return mx_ref.flush((rng.standard_normal(shape, dtype=np.float32) * np.exp2(rng.integers(-2, 3, shape[:-1] + (1,)))).astype(BF))
def wide(rng, *shape, cols=0):
    v = rng.standard_normal(shape, dtype=np.float32) * np.exp2(rng.integers(-12, 13, shape)).astype(np.float32)
    if cols: v *= np.repeat(np.exp2(rng.integers(-cols, cols + 1, shape[:-2] + (1, shape[-1] // 4))) * (rng.random(shape[:-2] + (1, shape[-1] // 4)) > 0.0625), 4, axis=-1).astype(np.float32)
    return mx_ref.flush(v.astype(BF))
T, K, O = 512, 256, 4
def setup_inputs(rng):
    u = np.zeros((128, 512), BF); u[:, :4] = f(rng, 128, 4)
    return {"x": f(rng, N, 128, 4 * T), "u": np.stack([u] * N), "w": f(rng, N, 128, 512 * O)}
def signs(d):
    return np.where(d["u"][0][:, :4].astype(np.float32) < 0, -1, 1).astype(np.float32)
def blocks(rng, n):
    return np.repeat(rng.permutation(16) < n, 8)
def plant(rng, d, n):
    for s in range(N):
        v = d["x"][s].astype(np.float32).reshape(128, T, 4)
        k = rng.permutation(T)[:n[s]]
        v[:, k] = np.abs(v[:, k]) * signs(d)[:, None] * np.float32(8)
        d["x"][s] = v.reshape(128, -1).astype(BF)
    return d
def setup_inputs_one(rng):
    d = setup_inputs(rng); return plant(rng, d, np.where(np.arange(N) == rng.integers(0, N), K, 0))
def setup_inputs_zeros(rng):
    d = setup_inputs(rng); m = blocks(rng, 2)
    d["u"][:, ~m] = 0
    k = rng.permutation(N * T); g = np.full(N * T, -1, np.float32)
    g[k[:K // 3]] = 1; g[k[K // 3:2 * (K // 3)]] = 0
    v = np.abs(d["x"][:, m].astype(np.float32)).reshape(N, -1, T, 4)
    d["x"][:, m] = (v * signs(d)[m][:, None] * g.reshape(N, 1, T, 1)).reshape(N, -1, 4 * T).astype(BF)
    return d
def setup_inputs_few(rng):
    d = setup_inputs(rng); p = rng.permutation(N); g = p[N - N // 2:]
    d["x"][g] = (-np.abs(d["x"][g].astype(np.float32)) * np.tile(signs(d), (1, T))).astype(BF)
    n = np.zeros(N, int); n[p[:2]] = [K * 3 // 5, K - K * 3 // 5]
    return plant(rng, d, n)
def setup_inputs_ties(rng):
    d = setup_inputs(rng); b = f(rng, 128, 4 * 20); m = blocks(rng, 4)
    d["u"][:, m] = 0
    d["x"] = np.stack([cols(b, rng.permutation(np.arange(T) % 20)) for r in range(N)])
    d["x"][:, m] = f(rng, N, 32, 4 * T); return d
def setup_inputs_spread(rng):
    d = setup_inputs(rng); d["x"] = wide(rng, N, 128, 4 * T, cols=8); return d
def check_inputs(d):
    b = []
    u = d["u"].astype(np.float32)
    if (u != u[:1]).any(): b.append("u_same")
    if (u[:, :, 4:] != 0).any(): b.append("u_zero")
    return b
def reference(x, u, w):
    s = np.stack([mx_ref.matmul(mx_ref.quantize(u[r]), mx_ref.quantize(x[r]))[0] for r in range(N)]).reshape(-1) + np.float32(0.0)
    best = np.lexsort((np.arange(N * T), -s))[:K]
    V = mx_ref.quantize(cols(np.concatenate(list(x), axis=1), best))
    y = np.zeros((N, 128, O * K), np.float32)
    for r in range(N):
        for o in range(O): y[r][:, K * o:K * o + K] = mx_ref.matmul(mx_ref.quantize(np.ascontiguousarray(w[r][:, 512 * o:512 * o + 512])), V)
    who = np.stack([best // T, best % T]).astype(np.float32)
    return {"y": y, "id": np.stack([who] * N)}

@@ -1,0 +1,255 @@
+from concourse.bass import DstId, RemoteDMATransfer
+from concourse.mybir import dt, AluOpType, ActivationFunctionType
+
+K, O = 256, 4
+H = 256
+SCRATCH = {"ps": ("psum", [128, 4096], "float32")}
+
+
+def _bufs(dtype, **widths):
+    for name, n in widths.items():
+        SCRATCH[name] = ("sbuf", [128, n], dtype)
+
+
+_bufs("float8_e4m3fn_x4", cx=512, cu=128, cw=512, c1=512, cr=256, c2=512, c3=256)
+_bufs("uint8", sx=512, su=128, sw=512, s1=512, sr=256, s2=512, s3=256)
+_bufs("bfloat16", xb=2048, wb=2048, ub=16, up=512, neg=128, dm=128, fl=2048, cs=256, f1=256)
+_bufs("float32", sc4=4, nd=4, th=512, pl=128, plt=128, pof=32, win=512, wm=256, ws=256, val=512, mk=256, rs=256, k16=16,
+      iot=512, who=1024, rv=256, g1=128, part=1, theirs=1, t512=1, h1=16, h2=16, colr=1024, e1=16, e2=16, e3=16, e4=16,
+      e5=16, e6=16, wo=256, co=256, ysb=1024)
+_bufs("int32", ip=32, i3=32, i15=16, c16=16, mi=256, mj=256, ri=256)
+_bufs("uint16", u4=32, pou=32, kr=16, l0=16, l1=16, l2=16, l3=16, q1=16, q2=16, eu=16)
+SEMAPHORES = ["cv", "ca", "ct", "cp", "du", "dx0", "dx1", "dw", "rel", "dy", "did",
+              "a1", "o1", "al", "ol", "a2", "o2", "am", "om"]
+STEP, TINY = 1.125 * 2.0 ** -24, 2.0 ** -124
+
+
+def rank_program(g, core, T, topo):
+    rank = T.rank_of(core)
+    if rank is None:
+        return
+    A, F = AluOpType, ActivationFunctionType
+    q = {"v": g.vector, "s": g.scalar, "t": g.tensor, "g": g, "y": g.sync}
+    cnt, seen = {}, {}
+
+    def inc(sem, ins, n=1):
+        ins.then_inc(T.sem[sem], n)
+        cnt[sem] = cnt.get(sem, 0) + n
+        return (sem, cnt[sem])
+
+    def wait(qn, *toks):
+        best = {}
+        for t in toks:
+            best[t[0]] = max(best.get(t[0], 0), t[1])
+        for sem, v in best.items():
+            if seen.get((qn, sem), 0) < v:
+                q[qn].wait_ge(T.sem[sem], v)
+                seen[(qn, sem)] = v
+
+    def vec(name, *args, after=()):
+        wait("v", *after)
+        calls = {"copy": g.vector.tensor_copy, "tt": g.vector.tensor_tensor, "ts": g.vector.tensor_scalar,
+                 "set": g.vector.memset, "scan": g.vector.tensor_tensor_scan, "tr": g.vector.transpose,
+                 "quant": g.vector.quantize_mx}
+        return inc("cv", calls[name](*args))
+
+    def act(out, in_, func, after=(), **kw):
+        wait("s", *after)
+        return inc("ca", g.scalar.activation(out, in_, func, **kw))
+
+    def mm(out, a, sa, b, sb, after=()):
+        wait("t", *after)
+        return inc("ct", g.tensor.matmul_mx(out, a, sa, b, sb, True, True))
+
+    lst = ["l0", "l1", "l2", "l3"]
+    mate, other = rank ^ 1, rank ^ 2
+    lower = rank < mate
+    a0 = 0 if lower else H
+    b0 = H - a0
+    f2 = 0 if rank < other else 1
+
+    du = inc("du", g.sync.dma_start(T.ub[:, 0:4], T.u[:, 0:4]), 16)
+    dx = [inc("dx%d" % h, g.sync.dma_start(T.xb[:, 1024 * h:1024 * h + 1024], T.x[:, 1024 * h:1024 * h + 1024]), 16)
+          for h in (0, 1)]
+    dw = inc("dw", g.sync.dma_start(T.wb[:], T.w[:]), 16)
+
+    vneg = vec("set", T.neg[:], -1.0)
+    vpl = vec("set", T.pl[:], 0.0)
+    f = {"allow_small_or_imprecise_dtypes": True}
+    pip = inc("cp", g.iota(T.ip[:], [[0, 32]], 0, 1))
+    wait("g", vneg)
+    pdm = inc("cp", g.affine_select(T.dm[:], T.neg[:], [[-1, 128]], A.is_gt, 0.0, 0, 1))
+    pmi = inc("cp", g.iota(T.mi[:], [[1, 256]], 0, 15))
+    pri = inc("cp", g.iota(T.ri[:], [[0, 16], [1, 16]], 0, 0))
+    pc16 = inc("cp", g.iota(T.c16[:], [[16, 16]], 0, 0))
+    pval = inc("cp", g.iota(T.val[:], [[1, 32], [32, 4], [128, 4]], 0, 0, **f))
+    piot = inc("cp", g.iota(T.iot[:], [[1, 512]], 0, 0, **f))
+    pwho = inc("cp", g.iota(T.who[:], [[1, 4], [0, 256]], 0, 0, **f))
+    v = vec("ts", T.i3[:], T.ip[:], 3, None, A.bitwise_and, after=[pip])
+    v15 = vec("ts", T.i15[:], T.ip[:, 0:16], 15, None, A.bitwise_and)
+    vu4 = vec("copy", T.u4[:], T.i3[:], after=[v])
+    v = vec("ts", T.mj[:], T.mi[:], 15, None, A.bitwise_and, after=[pmi])
+    vrs = vec("ts", T.rs[:], T.ri[:], 0, None, A.is_gt, after=[pri])
+    vmk = vec("ts", T.mk[:], T.mj[:], 0, None, A.is_equal, after=[v])
+    vk16 = vec("tt", T.k16[:], T.i15[:], T.c16[:], A.add, after=[v15, pc16])
+    vkr = vec("ts", T.kr[:], T.k16[:], -1.0, 255.0, A.mult, A.add, after=[vk16])
+
+    v = vec("copy", T.up[:], T.ub[:, 0:4].indirect(T.u4[:, 0:32]), after=[du, vu4])
+    vqu = vec("quant", T.cu[:], T.su[:], T.up[:], after=[v])
+
+    def score_half(c, s, h, toks):
+        wait("t", *toks)
+        for t in (2 * h, 2 * h + 1):
+            x = mm(T.ps[:, 512 * (2 + t):512 * (2 + t) + 128], c[:, 128 * t:128 * t + 128], s[:, 128 * t:128 * t + 128],
+                   T.cu[:], T.su[:])
+        r = mm(T.ps[:, 512 * h:512 * h + H], T.cu[:], T.su[:], c[:, H * h:H * h + H], s[:, H * h:H * h + H])
+        return x, r
+
+    def thresholds(h, tx):
+        src = T.ps[:, 512 * (2 + 2 * h):512 * (4 + 2 * h):512]
+        a = act(T.sc4[:, 2 * h:2 * h + 2], src, F.Copy, after=[tx])
+        b = act(T.nd[:, 2 * h:2 * h + 2], src, F.Abs, scale=STEP, bias=TINY)
+        return a, [act(T.th[:, 128 * t:128 * t + 128], T.dm[:], F.Identity, after=[a, b, pdm],
+                       scale=T.nd[:, t:t + 1], bias=T.sc4[:, t:t + 1]) for t in (2 * h, 2 * h + 1)]
+
+    def plain(t, j0, j1, toks=()):
+        p = 512 * (j0 // H) + j0 % H
+        return vec("ts", T.fl[:, 512 * t + j0:512 * t + j1], T.ps[:, p:p + j1 - j0], T.sc4[:, t:t + 1], None,
+                   A.is_ge if j1 <= 128 * t else A.is_gt, after=toks)
+
+    def diag(t, tok):
+        p = 512 * (t // 2) + 128 * (t % 2)
+        return vec("tt", T.fl[:, 640 * t:640 * t + 128], T.ps[:, p:p + 128], T.th[:, 128 * t:128 * t + 128], A.is_gt,
+                   after=[tok])
+
+    def total(t, *toks):
+        fl = T.fl[:, 512 * t:512 * t + 512]
+        return act(fl, fl, F.Copy, after=toks, accum_out=T.pl[:, 32 * t:32 * t + 1])
+
+    def own_half(h, sc, th, tr):
+        plain(2 * h, H * h + 128, H * h + 256, [sc, tr])
+        plain(2 * h + 1, H * h, H * h + 128)
+        diag(2 * h, th[0])
+        diag(2 * h + 1, th[1])
+
+    def finish(f, k, sck, thk, trk, out):
+        total(2 * f, plain(2 * f, H * k, H * k + H, [trk]), vpl)
+        total(2 * f + 1, plain(2 * f + 1, H * k, H * k + H))
+        plain(2 * k, H * f, H * f + H, [sck])
+        plain(2 * k, H * k + 128, H * k + 256)
+        s = total(2 * k, diag(2 * k, thk[0]))
+        t = 2 * k + 1
+        z = 512 * t
+        plain(t, H * f, H * f + H)
+        plain(t, H * k, H * k + 128)
+        e = diag(t, thk[1])
+        vec("scan", T.cs[:, 0:128], T.fl[:, z:z + 128], T.fl[:, z + 128:z + 256], 0.0, A.add, A.add, after=[e])
+        e = vec("scan", T.cs[:, 128:256], T.fl[:, z + 256:z + 384], T.fl[:, z + 384:z + 512], 0.0, A.add, A.add)
+        e = vec("tt", T.pl[:, 32 * t:32 * t + 1], T.cs[:, 127:128], T.cs[:, 255:256], A.add, after=[e])
+        e = vec("tr", T.plt[:], T.pl[:], after=[e, s])
+        for i in range(8):
+            qn = "y" if i % 2 == 0 else "s"
+            wait(qn, e)
+            r = inc("rel", q[qn].dma_start(T.pof[16 * i:16 * i + 16, :], T.plt[0:128:32, :]), 16)
+        e = vec("copy", T.pou[:], T.pof[:], after=[r])
+        e = vec("copy", T.win[:].indirect(T.pou[:]), T.val[:], after=[e, pval])
+        e = vec("tt", T.wm[:], T.win[:, 0:256], T.mk[:], A.mult, after=[e, vmk])
+        e = vec("scan", T.ws[:], T.rs[:], T.wm[:], 0.0, A.mult, A.add, after=[e, vrs])
+        return vec("copy", out[:], T.ws[:, 15:256:16], after=[e])
+
+    def pick(c_to, s_to, j, c, s, i0, i1, off, *toks):
+        v = vec("copy", c_to[:, j:j + K].bitcast(dt.uint32), c[:, i0:i1].bitcast(dt.uint32).indirect(off[:]), after=toks)
+        return v, act(s_to[:, j:j + K], s[:, i0:i1].indirect(off[:]), F.Copy, after=toks)
+
+    vq = vec("quant", T.cx[:, 0:H], T.sx[:, 0:H], T.xb[:, 0:1024], after=[dx[0]])
+    tx, tr0 = score_half(T.cx, T.sx, 0, [vqu, vq])
+    sc0, th0 = thresholds(0, tx)
+    vq = vec("quant", T.cx[:, H:2 * H], T.sx[:, H:2 * H], T.xb[:, 1024:2048], after=[dx[1]])
+    own_half(0, sc0, th0, tr0)
+    tx, tr1 = score_half(T.cx, T.sx, 1, [vq])
+    sc1, th1 = thresholds(1, tx)
+    mylist = T[lst[rank]]
+    ql = finish(0, 1, sc1, th1, tr1, mylist)
+    p1 = pick(T.c1, T.s1, a0, T.cx, T.sx, 0, 512, mylist, ql)
+
+    def send(c, s, j, to, arr, out, pk):
+        rid, pid, _ = topo.addr(T.cores[to])
+        m, n = topo.mask(core, T.cores[to]), len(topo.engines(core, T.cores[to]))
+        wait("g", pk[0])
+        cc = c[:, j:j + K].bitcast(dt.uint8)
+        g.remote_dma(cc, cc, T.sem[arr], T.sem[out], pid, rid, m)
+        wait("g", pk[1])
+        g.remote_dma(s[:, j:j + K], s[:, j:j + K], T.sem[arr], T.sem[out], pid, rid, m)
+        return (arr, 2 * n), (out, 2 * n)
+
+    arr1, out1 = send(T.c1, T.s1, a0, mate, "a1", "o1", p1)
+    tr, nl = [], 4
+    for i, r in enumerate(x for x in range(len(T.cores)) if x != rank):
+        rid, pid, _ = topo.addr(T.cores[r])
+        eng = topo.engines(core, T.cores[r])[nl * i:nl * i + nl]
+        tr.append(RemoteDMATransfer(dst_ids=[DstId(rid=rid, pnc=pid)], dma_engine_mask=sum(1 << e for e in eng),
+                                    remote_sem=T.sem.al, src=mylist[:], dst=mylist[:]))
+    wait("g", ql)
+    g.remote_dma_fused(tr, local_sem=T.sem.ol)
+    arrl, outl = ("al", nl * len(tr)), ("ol", nl * len(tr))
+
+    pr = pick(T.cr, T.sr, 0, T.c1, T.s1, a0, a0 + H, T.kr, vkr, *p1)
+    t = mm(T.ps[:, 3072:3328], T.cu[:], T.su[:], T.cr[:], T.sr[:], after=pr)
+    srv = act(T.rv[:], T.ps[:, 3072:3328], F.Copy, after=[t])
+    vw = vec("quant", T.cw[:], T.sw[:], T.wb[:], after=[dw])
+
+    t = mm(T.ps[:, 3584:3840], T.cu[:], T.su[:], T.c1[:, b0:b0 + H], T.s1[:, b0:b0 + H], after=[arr1])
+    rows = (T.rv[:], T.ps[:, 3584:3840]) if lower else (T.ps[:, 3584:3840], T.rv[:])
+    v = vec("tt", T.f1[:], rows[0], rows[1], A.is_lt, after=[t, srv])
+    mine = T.g1[:, 127:128]
+    vm = vec("scan", T.g1[:], T.f1[:, 0:128], T.f1[:, 128:256], 0.0, A.add, A.add, after=[v])
+    v = vec("ts", T.part[:], mine, -1.0, 256.0, A.mult, A.add, after=[vm])
+    v = vec("ts", T.h1[:], T.k16[:], T.part[:], mine, A.is_ge, A.mult, after=[v])
+    v = vec("tt", T.h2[:], T.h1[:], T.k16[:], A.add, after=[v])
+    v = vec("copy", T.q1[:], T.h2[:], after=[v])
+    p2 = pick(T.c2, T.s2, H * f2, T.c1, T.s1, 0, 512, T.q1, v, arr1, *p1)
+
+    arr2, out2 = send(T.c2, T.s2, H * f2, other, "a2", "o2", p2)
+    rid, pid, _ = topo.addr(T.cores[other])
+    eng = topo.engines(core, T.cores[other])[0:4]
+    wait("g", vm)
+    g.remote_dma(T.theirs[:], mine, T.sem.am, T.sem.om, pid, rid, sum(1 << e for e in eng))
+    arrm, outm = ("am", len(eng)), ("om", len(eng))
+
+    tx, trf = score_half(T.c2, T.s2, f2, p2)
+    scf, thf = thresholds(f2, tx)
+    own_half(f2, scf, thf, trf)
+    for i in range(4):
+        sid = act(T.colr[:, 256 * i:256 * i + 256], T.iot[:].indirect(T[lst[i]][:]), F.Copy,
+                  after=[piot, ql if i == rank else arrl])
+
+    tx, trk = score_half(T.c2, T.s2, 1 - f2, [arr2])
+    sck, thk = thresholds(1 - f2, tx)
+    v2 = finish(f2, 1 - f2, sck, thk, trk, T.q2)
+    p3 = pick(T.c3, T.s3, 0, T.c2, T.s2, 0, 512, T.q2, v2, arr2, *p2)
+
+    ty = [mm(T.ps[:, 512 * (2 + o):512 * (2 + o) + K], T.cw[:, 128 * o:128 * o + 128], T.sw[:, 128 * o:128 * o + 128],
+             T.c3[:], T.s3[:], after=[*p3, vw]) for o in range(O)]
+    ws = T.ws[:, 15:256:16]
+    mlo, mhi = (mine, T.theirs[:]) if f2 == 0 else (T.theirs[:], mine)
+    vec("ts", T.t512[:], mhi, -1.0, 512.0, A.mult, A.add, after=[arrm])
+    w = vec("ts", T.part[:], mlo, -1.0, 256.0, A.mult, A.add)
+    w1 = vec("ts", T.e1[:], ws, T.part[:], mlo, A.is_ge, A.mult, after=[w])
+    vec("ts", T.e2[:], ws, 256.0, T.part[:], A.is_ge, A.mult)
+    w3 = vec("ts", T.e3[:], ws, T.t512[:], mhi, A.is_ge, A.mult)
+    vec("tt", T.e4[:], ws, T.e1[:], A.add, after=[w1])
+    w = vec("tt", T.e5[:], T.e2[:], T.e3[:], A.add, after=[w3])
+    w = vec("tt", T.e6[:], T.e4[:], T.e5[:], A.add, after=[w])
+    w = vec("copy", T.eu[:], T.e6[:], after=[w])
+    for o in range(O):
+        src, out = T.ps[:, 512 * (2 + o):512 * (2 + o) + K], T.ysb[:, K * o:K * o + K]
+        wait("y", vec("copy", out, src, after=[ty[o]]) if o % 2 else act(out, src, F.Copy, after=[ty[o]]))
+        inc("dy", g.sync.dma_start(T.y[:, K * o:K * o + K], out), 16)
+    vco = vec("copy", T.co[:], T.colr[:].indirect(T.eu[:]), after=[w, sid])
+    swo = act(T.wo[:], T.who[:].indirect(T.eu[:]), F.Copy, after=[w, pwho])
+    wait("y", swo)
+    inc("did", g.sync.dma_start(T.id[0:1, :], T.wo[0:1, :]), 16)
+    wait("y", vco)
+    inc("did", g.sync.dma_start(T.id[1:2, :], T.co[0:1, :]), 16)
+
+    wait("g", out1, outl, out2, outm, arr1, arrl, arr2, arrm, *[(s, n) for s, n in cnt.items()])

@@ -3,6 +3,7 @@ from concourse.mybir import dt, AluOpType, ActivationFunctionType
 
 K, O = 256, 4
 H = 256
+B = 528
 SCRATCH = {"ps": ("psum", [128, 4096], "float32")}
 
 
@@ -11,15 +12,15 @@ def _bufs(dtype, **widths):
         SCRATCH[name] = ("sbuf", [128, n], dtype)
 
 
-_bufs("float8_e4m3fn_x4", cx=512, cu=128, cw=512, c1=512, cr=256, c2=512, c3=256)
-_bufs("uint8", sx=512, su=128, sw=512, s1=512, sr=256, s2=512, s3=256)
-_bufs("bfloat16", xb=2048, wb=2048, ub=16, up=512, neg=128, dm=128, fl=2048, cs=256, f1=256)
-_bufs("float32", sc4=4, nd=4, th=512, pl=128, plt=128, pof=32, win=512, wm=256, ws=256, val=512, mk=256, rs=256, k16=16,
-      iot=512, who=1024, rv=256, g1=128, part=1, theirs=1, t512=1, h1=16, h2=16, colr=1024, e1=16, e2=16, e3=16, e4=16,
-      e5=16, e6=16, wo=256, co=256, ysb=1024)
-_bufs("int32", ip=32, i3=32, i15=16, c16=16, mi=256, mj=256, ri=256)
-_bufs("uint16", u4=32, pou=32, kr=16, l0=16, l1=16, l2=16, l3=16, q1=16, q2=16, eu=16)
-SEMAPHORES = ["cv", "ca", "ct", "cp", "du", "dx0", "dx1", "dw", "rel", "dy", "did",
+_bufs("float8_e4m3fn_x4", cx=512, cu=128, cw=512, c1=512, cr=256, c2=512)
+_bufs("uint8", sx=512, su=128, sw=512, s1=512, sr=256, s2=512)
+_bufs("bfloat16", xb=2048, wb=2048, ub=16, up=512, neg=128, dm=128, fl=4 * B, cs=256, f1=256)
+_bufs("float32", sc4=4, nd=4, th=512, pl=4, ec=2, win=512, wt=256, x1=16, y1=16, x2=16, y2=16, gb=32, gt=32, xt=64, xo=64,
+      val=64, vb=64, hc=1, k16=16, k256=16, iot=512, rv=256, g1=128, part=1, theirs=1, npart=1, h1=16, h2=16, h3=16, h4=16,
+      colr=1024, colw=512, whow=512, wo=256, co=256, yy=2048, ysb=1024)
+_bufs("int32", ip=32, i3=32, i15=16, c16=16)
+_bufs("uint16", u4=32, pou=4, kr=16, ud=4, l0=16, l1=16, l2=16, l3=16, q1=16, q1o=16, q2=16)
+SEMAPHORES = ["cv", "ca", "ct", "cp", "du", "dx0", "dx1", "dw", "dy", "did",
               "a1", "o1", "al", "ol", "a2", "o2", "am", "om"]
 STEP, TINY = 1.125 * 2.0 ** -24, 2.0 ** -124
 
@@ -67,95 +68,117 @@ def rank_program(g, core, T, topo):
     a0 = 0 if lower else H
     b0 = H - a0
     f2 = 0 if rank < other else 1
+    k2 = 1 - f2
 
-    du = inc("du", g.sync.dma_start(T.ub[:, 0:4], T.u[:, 0:4]), 16)
+    du = inc("du", g.scalar.dma_start(T.ub[:, 0:4], T.u[:, 0:4]), 16)
     dx = [inc("dx%d" % h, g.sync.dma_start(T.xb[:, 1024 * h:1024 * h + 1024], T.x[:, 1024 * h:1024 * h + 1024]), 16)
           for h in (0, 1)]
     dw = inc("dw", g.sync.dma_start(T.wb[:], T.w[:]), 16)
 
     vneg = vec("set", T.neg[:], -1.0)
-    vpl = vec("set", T.pl[:], 0.0)
+    vwin = vec("set", T.win[:, 0:256], 0.0)
+    vgb = vec("set", T.gb[:], 0.0)
     f = {"allow_small_or_imprecise_dtypes": True}
     pip = inc("cp", g.iota(T.ip[:], [[0, 32]], 0, 1))
     wait("g", vneg)
     pdm = inc("cp", g.affine_select(T.dm[:], T.neg[:], [[-1, 128]], A.is_gt, 0.0, 0, 1))
-    pmi = inc("cp", g.iota(T.mi[:], [[1, 256]], 0, 15))
-    pri = inc("cp", g.iota(T.ri[:], [[0, 16], [1, 16]], 0, 0))
     pc16 = inc("cp", g.iota(T.c16[:], [[16, 16]], 0, 0))
-    pval = inc("cp", g.iota(T.val[:], [[1, 32], [32, 4], [128, 4]], 0, 0, **f))
+    pvb = inc("cp", g.iota(T.vb[:], [[128, 4], [1, 16]], 0, 0, **f))
     piot = inc("cp", g.iota(T.iot[:], [[1, 512]], 0, 0, **f))
-    pwho = inc("cp", g.iota(T.who[:], [[1, 4], [0, 256]], 0, 0, **f))
     v = vec("ts", T.i3[:], T.ip[:], 3, None, A.bitwise_and, after=[pip])
     v15 = vec("ts", T.i15[:], T.ip[:, 0:16], 15, None, A.bitwise_and)
     vu4 = vec("copy", T.u4[:], T.i3[:], after=[v])
-    v = vec("ts", T.mj[:], T.mi[:], 15, None, A.bitwise_and, after=[pmi])
-    vrs = vec("ts", T.rs[:], T.ri[:], 0, None, A.is_gt, after=[pri])
-    vmk = vec("ts", T.mk[:], T.mj[:], 0, None, A.is_equal, after=[v])
-    vk16 = vec("tt", T.k16[:], T.i15[:], T.c16[:], A.add, after=[v15, pc16])
-    vkr = vec("ts", T.kr[:], T.k16[:], -1.0, 255.0, A.mult, A.add, after=[vk16])
+    v = vec("tt", T.hc[:], T.ip[:, 0:1], T.i15[:, 0:1], A.subtract, after=[v15])
+    vec("copy", T.ud[:, 0:2], T.i15[:, 0:2])
+    vud = vec("ts", T.ud[:, 2:4], T.i15[:, 2:4], 16, None, A.add)
+    vk16 = vec("tt", T.k16[:], T.i15[:], T.c16[:], A.add, after=[pc16])
+    vec("ts", T.k256[:], T.k16[:], -256.0, None, A.add, after=[vk16])
+    vkr = vec("ts", T.kr[:], T.k16[:], -1.0, 255.0, A.mult, A.add)
+    vval = vec("ts", T.val[:], T.vb[:], T.hc[:], None, A.add, after=[pvb, v])
 
-    v = vec("copy", T.up[:], T.ub[:, 0:4].indirect(T.u4[:, 0:32]), after=[du, vu4])
-    vqu = vec("quant", T.cu[:], T.su[:], T.up[:], after=[v])
+    s = act(T.up[:, 256:512], T.ub[:, 0:4].indirect(T.u4[:, 16:32]), F.Copy, after=[du, vu4])
+    v = vec("copy", T.up[:, 0:256], T.ub[:, 0:4].indirect(T.u4[:, 0:16]), after=[du])
+    vqu = vec("quant", T.cu[:], T.su[:], T.up[:], after=[v, s])
 
     def score_half(c, s, h, toks):
         wait("t", *toks)
+        r = mm(T.ps[:, 512 * h:512 * h + H], T.cu[:], T.su[:], c[:, H * h:H * h + H], s[:, H * h:H * h + H])
         for t in (2 * h, 2 * h + 1):
             x = mm(T.ps[:, 512 * (2 + t):512 * (2 + t) + 128], c[:, 128 * t:128 * t + 128], s[:, 128 * t:128 * t + 128],
                    T.cu[:], T.su[:])
-        r = mm(T.ps[:, 512 * h:512 * h + H], T.cu[:], T.su[:], c[:, H * h:H * h + H], s[:, H * h:H * h + H])
         return x, r
 
-    def thresholds(h, tx):
+    def column(h, tx):
         src = T.ps[:, 512 * (2 + 2 * h):512 * (4 + 2 * h):512]
-        a = act(T.sc4[:, 2 * h:2 * h + 2], src, F.Copy, after=[tx])
-        b = act(T.nd[:, 2 * h:2 * h + 2], src, F.Abs, scale=STEP, bias=TINY)
-        return a, [act(T.th[:, 128 * t:128 * t + 128], T.dm[:], F.Identity, after=[a, b, pdm],
-                       scale=T.nd[:, t:t + 1], bias=T.sc4[:, t:t + 1]) for t in (2 * h, 2 * h + 1)]
+        return (act(T.sc4[:, 2 * h:2 * h + 2], src, F.Copy, after=[tx]),
+                act(T.nd[:, 2 * h:2 * h + 2], src, F.Abs, scale=STEP, bias=TINY))
 
-    def plain(t, j0, j1, toks=()):
+    def inside(h, sc):
+        return [act(T.th[:, 128 * t:128 * t + 128], T.dm[:], F.Identity, after=[*sc, pdm],
+                    scale=T.nd[:, t:t + 1], bias=T.sc4[:, t:t + 1]) for t in (2 * h, 2 * h + 1)]
+
+    def plain(t, j0, j1, at, toks=()):
         p = 512 * (j0 // H) + j0 % H
-        return vec("ts", T.fl[:, 512 * t + j0:512 * t + j1], T.ps[:, p:p + j1 - j0], T.sc4[:, t:t + 1], None,
+        return vec("ts", T.fl[:, B * t + at:B * t + at + j1 - j0], T.ps[:, p:p + j1 - j0], T.sc4[:, t:t + 1], None,
                    A.is_ge if j1 <= 128 * t else A.is_gt, after=toks)
 
-    def diag(t, tok):
+    def diag(t, at, tok):
         p = 512 * (t // 2) + 128 * (t % 2)
-        return vec("tt", T.fl[:, 640 * t:640 * t + 128], T.ps[:, p:p + 128], T.th[:, 128 * t:128 * t + 128], A.is_gt,
+        return vec("tt", T.fl[:, B * t + at:B * t + at + 128], T.ps[:, p:p + 128], T.th[:, 128 * t:128 * t + 128], A.is_gt,
                    after=[tok])
 
-    def total(t, *toks):
-        fl = T.fl[:, 512 * t:512 * t + 512]
-        return act(fl, fl, F.Copy, after=toks, accum_out=T.pl[:, 32 * t:32 * t + 1])
+    def total(t, i0, i1, out, *toks):
+        fl = T.fl[:, B * t + i0:B * t + i1]
+        return act(fl, fl, F.Copy, after=toks, accum_out=out)
 
     def own_half(h, sc, th, tr):
-        plain(2 * h, H * h + 128, H * h + 256, [sc, tr])
-        plain(2 * h + 1, H * h, H * h + 128)
-        diag(2 * h, th[0])
-        diag(2 * h + 1, th[1])
+        plain(2 * h, H * h + 128, H * h + 256, 128, [sc[0], tr])
+        plain(2 * h + 1, H * h, H * h + 128, 0)
+        return diag(2 * h, 0, th[0]), diag(2 * h + 1, 128, th[1])
 
-    def finish(f, k, sck, thk, trk, out):
-        total(2 * f, plain(2 * f, H * k, H * k + H, [trk]), vpl)
-        total(2 * f + 1, plain(2 * f + 1, H * k, H * k + H))
-        plain(2 * k, H * f, H * f + H, [sck])
-        plain(2 * k, H * k + 128, H * k + 256)
-        s = total(2 * k, diag(2 * k, thk[0]))
+    def finish(f, k, col, trk, out, early, beside_s, fill):
+        def step(*args, after=()):
+            e = vec(*args, after=after)
+            if fill:
+                fill.pop(0)()
+            return e
+
+        at = 272 if early else H
+        a = plain(2 * f, H * k, H * k + H, at, [trk])
+        b = plain(2 * f + 1, H * k, H * k + H, at)
+        lo, hi = (271, 528) if early else (0, 512)
+        th = inside(k, col)
+        for i, x in ((0, a), (1, b)):
+            total(2 * f + i, lo, hi, T.pl[:, 2 * f + i:2 * f + i + 1], x)
+        plain(2 * k, H * f, H * f + H, 0, [col[0]])
+        plain(2 * k, H * k + 128, H * k + 256, H + 128)
+        s = total(2 * k, 0, 512, T.pl[:, 2 * k:2 * k + 1], diag(2 * k, H, th[0]))
         t = 2 * k + 1
-        z = 512 * t
-        plain(t, H * f, H * f + H)
-        plain(t, H * k, H * k + 128)
-        e = diag(t, thk[1])
+        z = B * t
+        plain(t, H * f, H * f + H, 0)
+        plain(t, H * k, H * k + 128, H)
+        e = diag(t, H + 128, th[1])
+        beside_s()
         vec("scan", T.cs[:, 0:128], T.fl[:, z:z + 128], T.fl[:, z + 128:z + 256], 0.0, A.add, A.add, after=[e])
         e = vec("scan", T.cs[:, 128:256], T.fl[:, z + 256:z + 384], T.fl[:, z + 384:z + 512], 0.0, A.add, A.add)
-        e = vec("tt", T.pl[:, 32 * t:32 * t + 1], T.cs[:, 127:128], T.cs[:, 255:256], A.add, after=[e])
-        e = vec("tr", T.plt[:], T.pl[:], after=[e, s])
-        for i in range(8):
-            qn = "y" if i % 2 == 0 else "s"
-            wait(qn, e)
-            r = inc("rel", q[qn].dma_start(T.pof[16 * i:16 * i + 16, :], T.plt[0:128:32, :]), 16)
-        e = vec("copy", T.pou[:], T.pof[:], after=[r])
-        e = vec("copy", T.win[:].indirect(T.pou[:]), T.val[:], after=[e, pval])
-        e = vec("tt", T.wm[:], T.win[:, 0:256], T.mk[:], A.mult, after=[e, vmk])
-        e = vec("scan", T.ws[:], T.rs[:], T.wm[:], 0.0, A.mult, A.add, after=[e, vrs])
-        return vec("copy", out[:], T.ws[:, 15:256:16], after=[e])
+        vec("copy", T.pou[:, 2 * f:2 * f + 2], T.pl[:, 2 * f:2 * f + 2], after=[s])
+        vec("copy", T.pou[:, 2 * k:2 * k + 1], T.pl[:, 2 * k:2 * k + 1])
+        e = vec("ts", T.pou[:, t:t + 1], T.cs[:, 127:128], T.cs[:, 255:256], None, A.add, after=[e])
+        e = step("copy", T.win[:].indirect(T.pou[:]), T.val[:], after=[e, vval, vwin])
+        e = step("tr", T.wt[:], T.win[:, 0:256], after=[e])
+        for d in range(4):
+            e = vec("copy", T.x1[32 * d:32 * d + 32, :], T.wt[32 * (d ^ 1):32 * (d ^ 1) + 32, 0:256:16],
+                    after=[e] if d == 0 else [])
+        e = step("tt", T.y1[:], T.x1[:], T.wt[:, 0:256:16], A.add, after=[e])
+        vec("copy", T.x2[0:64, :], T.y1[64:128, :], after=[e])
+        e = vec("copy", T.x2[64:128, :], T.y1[0:64, :])
+        e = step("tt", T.y2[:], T.x2[:], T.y1[:], A.add, after=[e])
+        e = vec("tt", T.gb[:, 0:8], T.y2[:, 0:16:2], T.y2[:, 1:16:2], A.add, after=[e, vgb])
+        e = vec("tr", T.gt[:], T.gb[:], after=[e])
+        e = vec("copy", T.xt[:], T.gt[:].indirect(T.ud[:]), after=[e, vud])
+        e = vec("tr", T.xo[:], T.xt[:], after=[e])
+        vec("copy", out[:, 0:16:2], T.xo[:, 0:8], after=[e])
+        return vec("copy", out[:, 1:16:2], T.xo[:, 32:40])
 
     def pick(c_to, s_to, j, c, s, i0, i1, off, *toks):
         v = vec("copy", c_to[:, j:j + K].bitcast(dt.uint32), c[:, i0:i1].bitcast(dt.uint32).indirect(off[:]), after=toks)
@@ -163,13 +186,13 @@ def rank_program(g, core, T, topo):
 
     vq = vec("quant", T.cx[:, 0:H], T.sx[:, 0:H], T.xb[:, 0:1024], after=[dx[0]])
     tx, tr0 = score_half(T.cx, T.sx, 0, [vqu, vq])
-    sc0, th0 = thresholds(0, tx)
+    sc0 = column(0, tx)
+    th0 = inside(0, sc0)
     vq = vec("quant", T.cx[:, H:2 * H], T.sx[:, H:2 * H], T.xb[:, 1024:2048], after=[dx[1]])
     own_half(0, sc0, th0, tr0)
     tx, tr1 = score_half(T.cx, T.sx, 1, [vq])
-    sc1, th1 = thresholds(1, tx)
     mylist = T[lst[rank]]
-    ql = finish(0, 1, sc1, th1, tr1, mylist)
+    ql = finish(0, 1, column(1, tx), tr1, mylist, False, lambda: None, [])
     p1 = pick(T.c1, T.s1, a0, T.cx, T.sx, 0, 512, mylist, ql)
 
     def send(c, s, j, to, arr, out, pk):
@@ -193,21 +216,32 @@ def rank_program(g, core, T, topo):
     g.remote_dma_fused(tr, local_sem=T.sem.ol)
     arrl, outl = ("al", nl * len(tr)), ("ol", nl * len(tr))
 
+    def columns(r):
+        return act(T.colr[:, 256 * r:256 * r + 256], T.iot[:].indirect(T[lst[r]][:]), F.Copy,
+                   after=[piot, ql if r == rank else arrl])
+
     pr = pick(T.cr, T.sr, 0, T.c1, T.s1, a0, a0 + H, T.kr, vkr, *p1)
     t = mm(T.ps[:, 3072:3328], T.cu[:], T.su[:], T.cr[:], T.sr[:], after=pr)
     srv = act(T.rv[:], T.ps[:, 3072:3328], F.Copy, after=[t])
     vw = vec("quant", T.cw[:], T.sw[:], T.wb[:], after=[dw])
+    vwin = vec("set", T.win[:, 0:256], 0.0)
+    columns(rank)
 
     t = mm(T.ps[:, 3584:3840], T.cu[:], T.su[:], T.c1[:, b0:b0 + H], T.s1[:, b0:b0 + H], after=[arr1])
     rows = (T.rv[:], T.ps[:, 3584:3840]) if lower else (T.ps[:, 3584:3840], T.rv[:])
-    v = vec("tt", T.f1[:], rows[0], rows[1], A.is_lt, after=[t, srv])
+    v = vec("tt", T.f1[:], rows[0], rows[1], A.is_ge, after=[t, srv])
     mine = T.g1[:, 127:128]
-    vm = vec("scan", T.g1[:], T.f1[:, 0:128], T.f1[:, 128:256], 0.0, A.add, A.add, after=[v])
-    v = vec("ts", T.part[:], mine, -1.0, 256.0, A.mult, A.add, after=[vm])
-    v = vec("ts", T.h1[:], T.k16[:], T.part[:], mine, A.is_ge, A.mult, after=[v])
-    v = vec("tt", T.h2[:], T.h1[:], T.k16[:], A.add, after=[v])
-    v = vec("copy", T.q1[:], T.h2[:], after=[v])
-    p2 = pick(T.c2, T.s2, H * f2, T.c1, T.s1, 0, 512, T.q1, v, arr1, *p1)
+    vm = vec("scan", T.g1[:], T.f1[:, 0:128], T.f1[:, 128:256], -256.0, A.add, A.add, after=[v])
+
+    def choice1(m, h1, *toks):
+        return vec("ts", h1[:], T.k256[:], m, m, A.is_ge, A.mult, after=toks)
+
+    def choice2(h1, h2, *toks):
+        return vec("tt", h2[:], T.k16[:], h1[:], A.subtract, after=toks)
+
+    v = choice2(T.h1, T.h2, choice1(mine, T.h1, vm))
+    vc = vec("copy", T.q1[:], T.h2[:], after=[v])
+    p2 = pick(T.c2, T.s2, H * f2, T.c1, T.s1, 0, 512, T.q1, vc, arr1, *p1)
 
     arr2, out2 = send(T.c2, T.s2, H * f2, other, "a2", "o2", p2)
     rid, pid, _ = topo.addr(T.cores[other])
@@ -216,40 +250,66 @@ def rank_program(g, core, T, topo):
     g.remote_dma(T.theirs[:], mine, T.sem.am, T.sem.om, pid, rid, sum(1 << e for e in eng))
     arrm, outm = ("am", len(eng)), ("om", len(eng))
 
+    def products(h, banks, toks):
+        return [mm(T.ps[:, 512 * b:512 * b + H], T.cw[:, 128 * o:128 * o + 128], T.sw[:, 128 * o:128 * o + 128],
+                   T.c2[:, H * h:H * h + H], T.s2[:, H * h:H * h + H], after=toks) for o, b in enumerate(banks)]
+
+    def result(h, o, b):
+        return T.yy[:, 512 * o + H * h:512 * o + H * h + H], T.ps[:, 512 * b:512 * b + H]
+
+    def who(h, m, n, *toks):
+        e = vec("ts", n[:], m, 256.0, None, A.add, after=toks)
+        return vec("ts", T.whow[:, H * h:H * h + H], T.iot[:, 0:H], n[:], 2.0 * h, A.is_ge, A.add, after=[piot, e])
+
+    def col(h, lists, *toks):
+        return act(T.colw[:, H * h:H * h + H], T.colr[:, 512 * h:512 * h + 512].indirect(lists[:]), F.Copy, after=toks)
+
     tx, trf = score_half(T.c2, T.s2, f2, p2)
-    scf, thf = thresholds(f2, tx)
-    own_half(f2, scf, thf, trf)
-    for i in range(4):
-        sid = act(T.colr[:, 256 * i:256 * i + 256], T.iot[:].indirect(T[lst[i]][:]), F.Copy,
-                  after=[piot, ql if i == rank else arrl])
+    bf = [6, 7, 2 + 2 * k2, 3 + 2 * k2]
+    typ = products(f2, bf, [vw])
+    scf = column(f2, tx)
+    d = own_half(f2, scf, inside(f2, scf), trf)
+    for i in (0, 1):
+        s = total(2 * f2 + i, 0, H, T.ec[:, i:i + 1], d[i])
+        act(T.fl[:, B * (2 * f2 + i) + 271:B * (2 * f2 + i) + 272], T.ec[:, i:i + 1], F.Copy, after=[s])
+    done = [vec("copy", *result(f2, o, bf[o]), after=[typ[o]]) for o in range(O)]
+    who(f2, mine, T.part)
+    col(f2, T.q1, vc, columns(mate))
+    columns(other)
 
-    tx, trk = score_half(T.c2, T.s2, 1 - f2, [arr2])
-    sck, thk = thresholds(1 - f2, tx)
-    v2 = finish(f2, 1 - f2, sck, thk, trk, T.q2)
-    p3 = pick(T.c3, T.s3, 0, T.c2, T.s2, 0, 512, T.q2, v2, arr2, *p2)
+    tx, trk = score_half(T.c2, T.s2, k2, [arr2, *done])
+    colk = column(k2, tx)
+    bk = [6, 7, 2 + 2 * f2, 3 + 2 * f2]
+    tyq = products(k2, bk, [*scf])
+    last = {}
 
-    ty = [mm(T.ps[:, 512 * (2 + o):512 * (2 + o) + K], T.cw[:, 128 * o:128 * o + 128], T.sw[:, 128 * o:128 * o + 128],
-             T.c3[:], T.s3[:], after=[*p3, vw]) for o in range(O)]
-    ws = T.ws[:, 15:256:16]
-    mlo, mhi = (mine, T.theirs[:]) if f2 == 0 else (T.theirs[:], mine)
-    vec("ts", T.t512[:], mhi, -1.0, 512.0, A.mult, A.add, after=[arrm])
-    w = vec("ts", T.part[:], mlo, -1.0, 256.0, A.mult, A.add)
-    w1 = vec("ts", T.e1[:], ws, T.part[:], mlo, A.is_ge, A.mult, after=[w])
-    vec("ts", T.e2[:], ws, 256.0, T.part[:], A.is_ge, A.mult)
-    w3 = vec("ts", T.e3[:], ws, T.t512[:], mhi, A.is_ge, A.mult)
-    vec("tt", T.e4[:], ws, T.e1[:], A.add, after=[w1])
-    w = vec("tt", T.e5[:], T.e2[:], T.e3[:], A.add, after=[w3])
-    w = vec("tt", T.e6[:], T.e4[:], T.e5[:], A.add, after=[w])
-    w = vec("copy", T.eu[:], T.e6[:], after=[w])
+    def beside_s():
+        for o in range(O):
+            last["y"] = act(*result(k2, o, bk[o]), F.Copy, after=[tyq[o]])
+        last["c"] = columns(other ^ 1)
+
+    def fill1():
+        last["v"] = choice1(T.theirs[:], T.h3, arrm)
+
+    def fill2():
+        last["v"] = choice2(T.h3, T.h4, last["v"])
+
+    def fill3():
+        last["v"] = vec("copy", T.q1o[:], T.h4[:], after=[last["v"]])
+
+    v2 = finish(f2, k2, colk, trk, T.q2, True, beside_s, [fill1, fill2, fill3])
+    sid = col(k2, T.q1o, last["c"], last["v"])
+
     for o in range(O):
-        src, out = T.ps[:, 512 * (2 + o):512 * (2 + o) + K], T.ysb[:, K * o:K * o + K]
-        wait("y", vec("copy", out, src, after=[ty[o]]) if o % 2 else act(out, src, F.Copy, after=[ty[o]]))
+        src, out = T.yy[:, 512 * o:512 * o + 512].indirect(T.q2[:]), T.ysb[:, K * o:K * o + K]
+        toks = [v2, *done, last["y"]]
+        wait("y", vec("copy", out, src, after=toks) if o % 2 == 0 else act(out, src, F.Copy, after=toks))
         inc("dy", g.sync.dma_start(T.y[:, K * o:K * o + K], out), 16)
-    vco = vec("copy", T.co[:], T.colr[:].indirect(T.eu[:]), after=[w, sid])
-    swo = act(T.wo[:], T.who[:].indirect(T.eu[:]), F.Copy, after=[w, pwho])
-    wait("y", swo)
-    inc("did", g.sync.dma_start(T.id[0:1, :], T.wo[0:1, :]), 16)
-    wait("y", vco)
+    v = vec("copy", T.wo[:], T.whow[:].indirect(T.q2[:]), after=[who(k2, T.theirs[:], T.npart)])
+    s = act(T.co[:], T.colw[:].indirect(T.q2[:]), F.Copy, after=[sid])
+    wait("y", s)
     inc("did", g.sync.dma_start(T.id[1:2, :], T.co[0:1, :]), 16)
+    wait("y", v)
+    inc("did", g.sync.dma_start(T.id[0:1, :], T.wo[0:1, :]), 16)
 
     wait("g", out1, outl, out2, outm, arr1, arrl, arr2, arrm, *[(s, n) for s, n in cnt.items()])

@@ -14,11 +14,11 @@ def _bufs(dtype, **widths):
 
 _bufs("float8_e4m3fn_x4", cx=512, cu=128, cw=512, c1=512, cr=256, c2=512)
 _bufs("uint8", sx=512, su=128, sw=512, s1=512, sr=256, s2=512)
-_bufs("bfloat16", xb=2048, wb=2048, ub=16, up=512, neg=128, dm=128, fl=4 * B, cs=256, f1=256)
-_bufs("float32", sc4=4, nd=4, th=512, pl=4, ec=2, win=512, wt=256, x1=16, y1=16, x2=16, y2=16, gb=32, gt=32, xt=64, xo=64,
-      val=64, vb=64, hc=1, k16=16, k256=16, iot=512, rv=256, g1=128, part=1, theirs=1, npart=1, h1=16, h2=16, h3=16, h4=16,
-      colr=1024, colw=512, whow=512, wo=256, co=256, yy=2048, ysb=1024)
-_bufs("int32", ip=32, i3=32, i15=16, c16=16)
+_bufs("bfloat16", xb=2048, wb=2048, ub=16, up=512, neg=128, dm=128, fl=4 * B, cs=256, ce=256, f1=256)
+_bufs("float32", sc4=4, nd=4, th=512, pl=4, win=512, wt=256, z=64, zs=64, rz=64, gt=32, xt=64, xo=64,
+      val=64, vb=64, hc=1, k16=16, k256=16, iot=512, rv=256, g1=128, part=1, npart=1, h1=16, h2=16, h3=16, h4=16,
+      msg=3, tms=3, colr=1024, colw=512, whow=512, wo=256, co=256, yy=2048, ysb=1024)
+_bufs("int32", ip=32, i3=32, i15=16, c16=16, ri=64)
 _bufs("uint16", u4=32, pou=4, kr=16, ud=4, l0=16, l1=16, l2=16, l3=16, q1=16, q1o=16, q2=16)
 SEMAPHORES = ["cv", "ca", "ct", "cp", "du", "dx0", "dx1", "dw", "dy", "did",
               "a1", "o1", "al", "ol", "a2", "o2", "am", "om"]
@@ -77,13 +77,13 @@ def rank_program(g, core, T, topo):
 
     vneg = vec("set", T.neg[:], -1.0)
     vwin = vec("set", T.win[:, 0:256], 0.0)
-    vgb = vec("set", T.gb[:], 0.0)
     f = {"allow_small_or_imprecise_dtypes": True}
     pip = inc("cp", g.iota(T.ip[:], [[0, 32]], 0, 1))
     wait("g", vneg)
     pdm = inc("cp", g.affine_select(T.dm[:], T.neg[:], [[-1, 128]], A.is_gt, 0.0, 0, 1))
     pc16 = inc("cp", g.iota(T.c16[:], [[16, 16]], 0, 0))
     pvb = inc("cp", g.iota(T.vb[:], [[128, 4], [1, 16]], 0, 0, **f))
+    pri = inc("cp", g.iota(T.ri[:], [[0, 8], [1, 8]], 0, 0))
     piot = inc("cp", g.iota(T.iot[:], [[1, 512]], 0, 0, **f))
     v = vec("ts", T.i3[:], T.ip[:], 3, None, A.bitwise_and, after=[pip])
     v15 = vec("ts", T.i15[:], T.ip[:, 0:16], 15, None, A.bitwise_and)
@@ -95,6 +95,7 @@ def rank_program(g, core, T, topo):
     vec("ts", T.k256[:], T.k16[:], -256.0, None, A.add, after=[vk16])
     vkr = vec("ts", T.kr[:], T.k16[:], -1.0, 255.0, A.mult, A.add)
     vval = vec("ts", T.val[:], T.vb[:], T.hc[:], None, A.add, after=[pvb, v])
+    vrz = vec("ts", T.rz[:], T.ri[:], 0, None, A.is_gt, after=[pri])
 
     s = act(T.up[:, 256:512], T.ub[:, 0:4].indirect(T.u4[:, 16:32]), F.Copy, after=[du, vu4])
     v = vec("copy", T.up[:, 0:256], T.ub[:, 0:4].indirect(T.u4[:, 0:16]), after=[du])
@@ -109,12 +110,11 @@ def rank_program(g, core, T, topo):
         return x, r
 
     def column(h, tx):
-        src = T.ps[:, 512 * (2 + 2 * h):512 * (4 + 2 * h):512]
-        return (act(T.sc4[:, 2 * h:2 * h + 2], src, F.Copy, after=[tx]),
-                act(T.nd[:, 2 * h:2 * h + 2], src, F.Abs, scale=STEP, bias=TINY))
+        return act(T.sc4[:, 2 * h:2 * h + 2], T.ps[:, 512 * (2 + 2 * h):512 * (4 + 2 * h):512], F.Copy, after=[tx])
 
     def inside(h, sc):
-        return [act(T.th[:, 128 * t:128 * t + 128], T.dm[:], F.Identity, after=[*sc, pdm],
+        n = act(T.nd[:, 2 * h:2 * h + 2], T.ps[:, 512 * (2 + 2 * h):512 * (4 + 2 * h):512], F.Abs, scale=STEP, bias=TINY)
+        return [act(T.th[:, 128 * t:128 * t + 128], T.dm[:], F.Identity, after=[sc, n, pdm],
                     scale=T.nd[:, t:t + 1], bias=T.sc4[:, t:t + 1]) for t in (2 * h, 2 * h + 1)]
 
     def plain(t, j0, j1, at, toks=()):
@@ -127,58 +127,86 @@ def rank_program(g, core, T, topo):
         return vec("tt", T.fl[:, B * t + at:B * t + at + 128], T.ps[:, p:p + 128], T.th[:, 128 * t:128 * t + 128], A.is_gt,
                    after=[tok])
 
-    def total(t, i0, i1, out, *toks):
+    def total(t, i0, i1, tok, out=None):
         fl = T.fl[:, B * t + i0:B * t + i1]
-        return act(fl, fl, F.Copy, after=toks, accum_out=out)
+        return act(fl, fl, F.Copy, after=[tok], accum_out=T.pl[:, t:t + 1] if out is None else out)
+
+    def halves(t, i, cs, j, tok):
+        z = B * t + i
+        return vec("scan", cs[:, j:j + 128], T.fl[:, z:z + 128], T.fl[:, z + 128:z + 256], 0.0, A.add, A.add, after=[tok])
 
     def own_half(h, sc, th, tr):
-        plain(2 * h, H * h + 128, H * h + 256, 128, [sc[0], tr])
+        plain(2 * h, H * h + 128, H * h + 256, 128, [sc, tr])
         plain(2 * h + 1, H * h, H * h + 128, 0)
         return diag(2 * h, 0, th[0]), diag(2 * h + 1, 128, th[1])
 
-    def finish(f, k, col, trk, out, early, beside_s, fill):
+    def cross(t, h, at, toks=()):
+        return plain(t, H * h, H * h + H, at, toks)
+
+    def pou(t, n=1):
+        return T.pou[:, t:t + n]
+
+    def places_first(f, k, sc, trk):
+        a = cross(2 * f, k, H, [trk])
+        b = cross(2 * f + 1, k, H)
+        th = inside(k, sc)
+        s0 = total(2 * f, 0, 512, a)
+        cross(2 * k, f, 0, [sc])
+        halves(2 * f + 1, 0, T.ce, 0, b)
+        b = halves(2 * f + 1, H, T.ce, 128, b)
+        plain(2 * k, H * k + 128, H * k + 256, H + 128)
+        s1 = total(2 * k, 0, 512, diag(2 * k, H, th[0]))
+        t = 2 * k + 1
+        cross(t, f, 0)
+        plain(t, H * k, H * k + 128, H)
+        e = diag(t, H + 128, th[1])
+        vec("ts", pou(2 * f + 1), T.ce[:, 127:128], T.ce[:, 255:256], None, A.add, after=[b])
+        vec("copy", pou(2 * f), T.pl[:, 2 * f:2 * f + 1], after=[s0])
+        halves(t, 0, T.cs, 0, e)
+        e = halves(t, H, T.cs, 128, e)
+        vec("copy", pou(2 * k), T.pl[:, 2 * k:2 * k + 1], after=[s1])
+        return vec("ts", pou(t), T.cs[:, 127:128], T.cs[:, 255:256], None, A.add, after=[e])
+
+    def places_last(f, k, sc, trk, arrm, beside):
+        a = cross(2 * f, k, 272, [trk])
+        b = cross(2 * f + 1, k, 272)
+        total(2 * f, 271, 528, a)
+        s0 = total(2 * f + 1, 271, 528, b)
+        s1 = total(2 * k, 0, H, cross(2 * k, f, 0, [sc]))
+        e = cross(2 * k + 1, f, 0)
+        beside()
+        e = halves(2 * k + 1, 0, T.cs, 0, e)
+        vec("copy", pou(2 * f, 2), T.pl[:, 2 * f:2 * f + 2], after=[s0])
+        vec("ts", pou(2 * k), T.pl[:, 2 * k:2 * k + 1], T.tms[:, 1:2], None, A.add, after=[s1, arrm])
+        return vec("ts", pou(2 * k + 1), T.cs[:, 127:128], T.tms[:, 2:3], None, A.add, after=[e])
+
+    def to_list(e, out, fill):
         def step(*args, after=()):
             e = vec(*args, after=after)
             if fill:
                 fill.pop(0)()
             return e
 
-        at = 272 if early else H
-        a = plain(2 * f, H * k, H * k + H, at, [trk])
-        b = plain(2 * f + 1, H * k, H * k + H, at)
-        lo, hi = (271, 528) if early else (0, 512)
-        th = inside(k, col)
-        for i, x in ((0, a), (1, b)):
-            total(2 * f + i, lo, hi, T.pl[:, 2 * f + i:2 * f + i + 1], x)
-        plain(2 * k, H * f, H * f + H, 0, [col[0]])
-        plain(2 * k, H * k + 128, H * k + 256, H + 128)
-        s = total(2 * k, 0, 512, T.pl[:, 2 * k:2 * k + 1], diag(2 * k, H, th[0]))
-        t = 2 * k + 1
-        z = B * t
-        plain(t, H * f, H * f + H, 0)
-        plain(t, H * k, H * k + 128, H)
-        e = diag(t, H + 128, th[1])
-        beside_s()
-        vec("scan", T.cs[:, 0:128], T.fl[:, z:z + 128], T.fl[:, z + 128:z + 256], 0.0, A.add, A.add, after=[e])
-        e = vec("scan", T.cs[:, 128:256], T.fl[:, z + 256:z + 384], T.fl[:, z + 384:z + 512], 0.0, A.add, A.add)
-        vec("copy", T.pou[:, 2 * f:2 * f + 2], T.pl[:, 2 * f:2 * f + 2], after=[s])
-        vec("copy", T.pou[:, 2 * k:2 * k + 1], T.pl[:, 2 * k:2 * k + 1])
-        e = vec("ts", T.pou[:, t:t + 1], T.cs[:, 127:128], T.cs[:, 255:256], None, A.add, after=[e])
         e = step("copy", T.win[:].indirect(T.pou[:]), T.val[:], after=[e, vval, vwin])
         e = step("tr", T.wt[:], T.win[:, 0:256], after=[e])
+
+        def run(d, n, src, j):
+            return T.z[32 * d:32 * d + n, j:64:4], T.wt[32 * src:32 * src + n, 0:256:16]
+
         for d in range(4):
-            e = vec("copy", T.x1[32 * d:32 * d + 32, :], T.wt[32 * (d ^ 1):32 * (d ^ 1) + 32, 0:256:16],
-                    after=[e] if d == 0 else [])
-        e = step("tt", T.y1[:], T.x1[:], T.wt[:, 0:256:16], A.add, after=[e])
-        vec("copy", T.x2[0:64, :], T.y1[64:128, :], after=[e])
-        e = vec("copy", T.x2[64:128, :], T.y1[0:64, :])
-        e = step("tt", T.y2[:], T.x2[:], T.y1[:], A.add, after=[e])
-        e = vec("tt", T.gb[:, 0:8], T.y2[:, 0:16:2], T.y2[:, 1:16:2], A.add, after=[e, vgb])
-        e = vec("tr", T.gt[:], T.gb[:], after=[e])
+            s = act(*run(d, 32, d ^ 3, 3), F.Copy, after=[e])
+        s = act(*run(3, 32, 2, 2), F.Copy)
+        vec("copy", *run(0, 128, 0, 0), after=[e])
+        vec("copy", *run(0, 64, 2, 1))
+        vec("copy", *run(2, 64, 0, 1))
+        for d in range(3):
+            e = vec("copy", *run(d, 32, d ^ 1, 2))
+        e = step("scan", T.zs[:], T.rz[:], T.z[:], 0.0, A.mult, A.add, after=[e, s, vrz])
+        e = vec("tr", T.gt[:], T.zs[:, 1:64:2], after=[e])
         e = vec("copy", T.xt[:], T.gt[:].indirect(T.ud[:]), after=[e, vud])
         e = vec("tr", T.xo[:], T.xt[:], after=[e])
-        vec("copy", out[:, 0:16:2], T.xo[:, 0:8], after=[e])
-        return vec("copy", out[:, 1:16:2], T.xo[:, 32:40])
+        vec("copy", out[:, 0:16:2], T.xo[:, 3:32:4], after=[e])
+        return vec("copy", out[:, 1:16:2], T.xo[:, 35:64:4])
 
     def pick(c_to, s_to, j, c, s, i0, i1, off, *toks):
         v = vec("copy", c_to[:, j:j + K].bitcast(dt.uint32), c[:, i0:i1].bitcast(dt.uint32).indirect(off[:]), after=toks)
@@ -192,7 +220,7 @@ def rank_program(g, core, T, topo):
     own_half(0, sc0, th0, tr0)
     tx, tr1 = score_half(T.cx, T.sx, 1, [vq])
     mylist = T[lst[rank]]
-    ql = finish(0, 1, column(1, tx), tr1, mylist, False, lambda: None, [])
+    ql = to_list(places_first(0, 1, column(1, tx), tr1), mylist, [])
     p1 = pick(T.c1, T.s1, a0, T.cx, T.sx, 0, 512, mylist, ql)
 
     def send(c, s, j, to, arr, out, pk):
@@ -242,13 +270,9 @@ def rank_program(g, core, T, topo):
     v = choice2(T.h1, T.h2, choice1(mine, T.h1, vm))
     vc = vec("copy", T.q1[:], T.h2[:], after=[v])
     p2 = pick(T.c2, T.s2, H * f2, T.c1, T.s1, 0, 512, T.q1, vc, arr1, *p1)
+    vmsg = vec("copy", T.msg[:, 0:1], mine)
 
     arr2, out2 = send(T.c2, T.s2, H * f2, other, "a2", "o2", p2)
-    rid, pid, _ = topo.addr(T.cores[other])
-    eng = topo.engines(core, T.cores[other])[0:4]
-    wait("g", vm)
-    g.remote_dma(T.theirs[:], mine, T.sem.am, T.sem.om, pid, rid, sum(1 << e for e in eng))
-    arrm, outm = ("am", len(eng)), ("om", len(eng))
 
     def products(h, banks, toks):
         return [mm(T.ps[:, 512 * b:512 * b + H], T.cw[:, 128 * o:128 * o + 128], T.sw[:, 128 * o:128 * o + 128],
@@ -268,28 +292,33 @@ def rank_program(g, core, T, topo):
     bf = [6, 7, 2 + 2 * k2, 3 + 2 * k2]
     typ = products(f2, bf, [vw])
     scf = column(f2, tx)
-    d = own_half(f2, scf, inside(f2, scf), trf)
+    thf = inside(f2, scf)
+    d = own_half(f2, scf, thf, trf)
+    st = [total(2 * f2 + i, 0, H, d[i], T.msg[:, 1 + i:2 + i]) for i in (0, 1)]
+    wait("g", vmsg, *st)
+    rid, pid, _ = topo.addr(T.cores[other])
+    eng = topo.engines(core, T.cores[other])[0:4]
+    g.remote_dma(T.tms[:], T.msg[:], T.sem.am, T.sem.om, pid, rid, sum(1 << e for e in eng))
+    arrm, outm = ("am", len(eng)), ("om", len(eng))
     for i in (0, 1):
-        s = total(2 * f2 + i, 0, H, T.ec[:, i:i + 1], d[i])
-        act(T.fl[:, B * (2 * f2 + i) + 271:B * (2 * f2 + i) + 272], T.ec[:, i:i + 1], F.Copy, after=[s])
+        act(T.fl[:, B * (2 * f2 + i) + 271:B * (2 * f2 + i) + 272], T.msg[:, 1 + i:2 + i], F.Copy, after=[st[i]])
     done = [vec("copy", *result(f2, o, bf[o]), after=[typ[o]]) for o in range(O)]
     who(f2, mine, T.part)
     col(f2, T.q1, vc, columns(mate))
     columns(other)
 
     tx, trk = score_half(T.c2, T.s2, k2, [arr2, *done])
-    colk = column(k2, tx)
+    sck = column(k2, tx)
     bk = [6, 7, 2 + 2 * f2, 3 + 2 * f2]
-    tyq = products(k2, bk, [*scf])
+    tyq = products(k2, bk, [scf, *thf])
     last = {}
 
-    def beside_s():
-        for o in range(O):
-            last["y"] = act(*result(k2, o, bk[o]), F.Copy, after=[tyq[o]])
-        last["c"] = columns(other ^ 1)
+    def beside():
+        for o in range(3):
+            act(*result(k2, o, bk[o]), F.Copy, after=[tyq[o]])
 
     def fill1():
-        last["v"] = choice1(T.theirs[:], T.h3, arrm)
+        last["v"] = choice1(T.tms[:, 0:1], T.h3, arrm)
 
     def fill2():
         last["v"] = choice2(T.h3, T.h4, last["v"])
@@ -297,15 +326,16 @@ def rank_program(g, core, T, topo):
     def fill3():
         last["v"] = vec("copy", T.q1o[:], T.h4[:], after=[last["v"]])
 
-    v2 = finish(f2, k2, colk, trk, T.q2, True, beside_s, [fill1, fill2, fill3])
-    sid = col(k2, T.q1o, last["c"], last["v"])
+    v2 = to_list(places_last(f2, k2, sck, trk, arrm, beside), T.q2, [fill1, fill2, fill3])
+    sy = act(*result(k2, 3, bk[3]), F.Copy, after=[tyq[3]])
+    sid = col(k2, T.q1o, columns(other ^ 1), last["v"])
 
     for o in range(O):
         src, out = T.yy[:, 512 * o:512 * o + 512].indirect(T.q2[:]), T.ysb[:, K * o:K * o + K]
-        toks = [v2, *done, last["y"]]
+        toks = [v2, *done, sy]
         wait("y", vec("copy", out, src, after=toks) if o % 2 == 0 else act(out, src, F.Copy, after=toks))
         inc("dy", g.sync.dma_start(T.y[:, K * o:K * o + K], out), 16)
-    v = vec("copy", T.wo[:], T.whow[:].indirect(T.q2[:]), after=[who(k2, T.theirs[:], T.npart)])
+    v = vec("copy", T.wo[:], T.whow[:].indirect(T.q2[:]), after=[who(k2, T.tms[:, 0:1], T.npart)])
     s = act(T.co[:], T.colw[:].indirect(T.q2[:]), F.Copy, after=[sid])
     wait("y", s)
     inc("did", g.sync.dma_start(T.id[1:2, :], T.co[0:1, :]), 16)

@@ -3,7 +3,6 @@ from concourse.mybir import dt, AluOpType, ActivationFunctionType
 
 K, O = 256, 4
 H = 256
-B = 528
 SCRATCH = {"ps": ("psum", [128, 4096], "float32")}
 
 
@@ -14,14 +13,14 @@ def _bufs(dtype, **widths):
 
 _bufs("float8_e4m3fn_x4", cx=512, cu=128, cw=512, c1=512, cr=256, c2=512)
 _bufs("uint8", sx=512, su=128, sw=512, s1=512, sr=256, s2=512)
-_bufs("bfloat16", xb=2048, wb=2048, ub=16, up=512, neg=128, dm=128, fl=4 * B, cs=256, ce=256, f1=256)
-_bufs("float32", sc4=4, nd=4, th=512, pl=4, win=512, wt=256, z=64, zs=64, rz=64, gt=32, xt=64, xo=64,
-      val=64, vb=64, hc=1, k16=16, k256=16, iot=512, rv=256, g1=128, part=1, npart=1, h1=16, h2=16, h3=16, h4=16,
-      msg=3, tms=3, colr=1024, colw=512, whow=512, wo=256, co=256, yy=2048, ysb=1024)
-_bufs("int32", ip=32, i3=32, i15=16, c16=16, ri=64)
-_bufs("uint16", u4=32, pou=4, kr=16, ud=4, l0=16, l1=16, l2=16, l3=16, q1=16, q1o=16, q2=16)
+_bufs("bfloat16", xb=2048, wb=2048, ub=16, up=512, neg=128, dm=128, fl=2048, cs=256, ce=256, f1=256, g1=128,
+      val=64, win=544, wt=544, z=136, zs=136, rz=136)
+_bufs("float32", sc4=4, nd=4, th=512, pl=4, vb=64, hc=1, fx=1, fy=1, fz=1, fw=1, k16=16, k256=16, iot=512, rv=256,
+      h1=16, h2=16, h3=16, h4=16, mn=1, tmn=1, msg=2, tms=2, colr=1024, colw=512, idf=64, yy=2048, ysb=1024)
+_bufs("int32", ip=32, i3=32, i15=16, c16=16, ri=136, y17=1, a14=1, a112=1, idi=32, idv=64)
+_bufs("uint16", u4=32, pou=4, kr=16, fo=2, fi=2, sel=16, l0=16, l1=16, l2=16, l3=16, q1=16, q1o=16, q2=16)
 SEMAPHORES = ["cv", "ca", "ct", "cp", "du", "dx0", "dx1", "dw", "dy", "did",
-              "a1", "o1", "al", "ol", "a2", "o2", "am", "om"]
+              "a1", "o1", "al0", "al1", "al2", "al3", "ol", "a2", "o2", "an", "on", "am", "om"]
 STEP, TINY = 1.125 * 2.0 ** -24, 2.0 ** -124
 
 
@@ -76,38 +75,48 @@ def rank_program(g, core, T, topo):
     dw = inc("dw", g.sync.dma_start(T.wb[:], T.w[:]), 16)
 
     vneg = vec("set", T.neg[:], -1.0)
-    vwin = vec("set", T.win[:, 0:256], 0.0)
     f = {"allow_small_or_imprecise_dtypes": True}
     pip = inc("cp", g.iota(T.ip[:], [[0, 32]], 0, 1))
     wait("g", vneg)
     pdm = inc("cp", g.affine_select(T.dm[:], T.neg[:], [[-1, 128]], A.is_gt, 0.0, 0, 1))
-    pc16 = inc("cp", g.iota(T.c16[:], [[16, 16]], 0, 0))
+    pri = inc("cp", g.iota(T.ri[:], [[0, 17], [1, 8]], 0, 0))
     pvb = inc("cp", g.iota(T.vb[:], [[128, 4], [1, 16]], 0, 0, **f))
-    pri = inc("cp", g.iota(T.ri[:], [[0, 8], [1, 8]], 0, 0))
+    pc16 = inc("cp", g.iota(T.c16[:], [[16, 16]], 0, 0))
     piot = inc("cp", g.iota(T.iot[:], [[1, 512]], 0, 0, **f))
     v = vec("ts", T.i3[:], T.ip[:], 3, None, A.bitwise_and, after=[pip])
     v15 = vec("ts", T.i15[:], T.ip[:, 0:16], 15, None, A.bitwise_and)
+    for out, bits in ((T.y17, 17), (T.a14, 14), (T.a112, 112)):
+        va = vec("ts", out[:], T.ip[:, 0:1], bits, None, A.bitwise_and)
     vu4 = vec("copy", T.u4[:], T.i3[:], after=[v])
-    v = vec("tt", T.hc[:], T.ip[:, 0:1], T.i15[:, 0:1], A.subtract, after=[v15])
-    vec("copy", T.ud[:, 0:2], T.i15[:, 0:2])
-    vud = vec("ts", T.ud[:, 2:4], T.i15[:, 2:4], 16, None, A.add)
-    vk16 = vec("tt", T.k16[:], T.i15[:], T.c16[:], A.add, after=[pc16])
-    vec("ts", T.k256[:], T.k16[:], -256.0, None, A.add, after=[vk16])
-    vkr = vec("ts", T.kr[:], T.k16[:], -1.0, 255.0, A.mult, A.add)
-    vval = vec("ts", T.val[:], T.vb[:], T.hc[:], None, A.add, after=[pvb, v])
-    vrz = vec("ts", T.rz[:], T.ri[:], 0, None, A.is_gt, after=[pri])
-
     s = act(T.up[:, 256:512], T.ub[:, 0:4].indirect(T.u4[:, 16:32]), F.Copy, after=[du, vu4])
-    v = vec("copy", T.up[:, 0:256], T.ub[:, 0:4].indirect(T.u4[:, 0:16]), after=[du])
+    v = vec("copy", T.up[:, 0:256], T.ub[:, 0:4].indirect(T.u4[:, 0:16]), after=[du, vu4])
     vqu = vec("quant", T.cu[:], T.su[:], T.up[:], after=[v, s])
+    vwin = vec("set", T.win[:, 0:304], 0.0)
+    vec("tt", T.hc[:], T.ip[:, 0:1], T.i15[:, 0:1], A.subtract, after=[v15])
+    vec("ts", T.fx[:], T.y17[:], 1, 72.0, A.is_equal, A.mult, after=[va])
+    vec("ts", T.fy[:], T.y17[:], 16, 64.0, A.is_equal, A.mult)
+    vec("ts", T.fz[:], T.a14[:], 4.0, 7.0, A.mult, A.add)
+    vf = vec("ts", T.fw[:], T.a112[:], 0.5, 7.0, A.mult, A.add)
 
-    def score_half(c, s, h, toks):
+    def constants():
+        vec("ts", T.fo[:, 0:1], T.fx[:], T.fy[:], T.fz[:], A.add, A.add, after=[vf])
+        vfo = vec("ts", T.fi[:, 0:1], T.fx[:], T.fy[:], T.fw[:], A.add, A.add)
+        vrz = vec("ts", T.rz[:], T.ri[:], 0, None, A.is_gt, after=[pri])
+        vval = vec("ts", T.val[:], T.vb[:], T.hc[:], -256.0, A.add, A.add, after=[pvb, vf])
+        vk16 = vec("tt", T.k16[:], T.i15[:], T.c16[:], A.add, after=[pc16])
+        return vfo, vrz, vval, vk16
+
+    def score_half(c, s, h, toks, row_first, later=()):
+        def row():
+            return mm(T.ps[:, 512 * h:512 * h + H], T.cu[:], T.su[:], c[:, H * h:H * h + H], s[:, H * h:H * h + H])
+
         wait("t", *toks)
-        r = mm(T.ps[:, 512 * h:512 * h + H], T.cu[:], T.su[:], c[:, H * h:H * h + H], s[:, H * h:H * h + H])
+        r = row() if row_first else None
+        wait("t", *later)
         for t in (2 * h, 2 * h + 1):
             x = mm(T.ps[:, 512 * (2 + t):512 * (2 + t) + 128], c[:, 128 * t:128 * t + 128], s[:, 128 * t:128 * t + 128],
                    T.cu[:], T.su[:])
-        return x, r
+        return x, r or row()
 
     def column(h, tx):
         return act(T.sc4[:, 2 * h:2 * h + 2], T.ps[:, 512 * (2 + 2 * h):512 * (4 + 2 * h):512], F.Copy, after=[tx])
@@ -119,20 +128,20 @@ def rank_program(g, core, T, topo):
 
     def plain(t, j0, j1, at, toks=()):
         p = 512 * (j0 // H) + j0 % H
-        return vec("ts", T.fl[:, B * t + at:B * t + at + j1 - j0], T.ps[:, p:p + j1 - j0], T.sc4[:, t:t + 1], None,
+        return vec("ts", T.fl[:, 512 * t + at:512 * t + at + j1 - j0], T.ps[:, p:p + j1 - j0], T.sc4[:, t:t + 1], None,
                    A.is_ge if j1 <= 128 * t else A.is_gt, after=toks)
 
     def diag(t, at, tok):
         p = 512 * (t // 2) + 128 * (t % 2)
-        return vec("tt", T.fl[:, B * t + at:B * t + at + 128], T.ps[:, p:p + 128], T.th[:, 128 * t:128 * t + 128], A.is_gt,
-                   after=[tok])
+        return vec("tt", T.fl[:, 512 * t + at:512 * t + at + 128], T.ps[:, p:p + 128], T.th[:, 128 * t:128 * t + 128],
+                   A.is_gt, after=[tok])
 
     def total(t, i0, i1, tok, out=None):
-        fl = T.fl[:, B * t + i0:B * t + i1]
+        fl = T.fl[:, 512 * t + i0:512 * t + i1]
         return act(fl, fl, F.Copy, after=[tok], accum_out=T.pl[:, t:t + 1] if out is None else out)
 
     def halves(t, i, cs, j, tok):
-        z = B * t + i
+        z = 512 * t + i
         return vec("scan", cs[:, j:j + 128], T.fl[:, z:z + 128], T.fl[:, z + 128:z + 256], 0.0, A.add, A.add, after=[tok])
 
     def own_half(h, sc, th, tr):
@@ -157,41 +166,41 @@ def rank_program(g, core, T, topo):
         plain(2 * k, H * k + 128, H * k + 256, H + 128)
         s1 = total(2 * k, 0, 512, diag(2 * k, H, th[0]))
         t = 2 * k + 1
-        cross(t, f, 0)
+        c = cross(t, f, 0)
         plain(t, H * k, H * k + 128, H)
+        halves(t, 0, T.cs, 0, c)
         e = diag(t, H + 128, th[1])
         vec("ts", pou(2 * f + 1), T.ce[:, 127:128], T.ce[:, 255:256], None, A.add, after=[b])
         vec("copy", pou(2 * f), T.pl[:, 2 * f:2 * f + 1], after=[s0])
-        halves(t, 0, T.cs, 0, e)
         e = halves(t, H, T.cs, 128, e)
         vec("copy", pou(2 * k), T.pl[:, 2 * k:2 * k + 1], after=[s1])
         return vec("ts", pou(t), T.cs[:, 127:128], T.cs[:, 255:256], None, A.add, after=[e])
 
-    def places_last(f, k, sc, trk, arrm, beside):
-        a = cross(2 * f, k, 272, [trk])
-        b = cross(2 * f + 1, k, 272)
-        total(2 * f, 271, 528, a)
-        s0 = total(2 * f + 1, 271, 528, b)
+    def places_last(f, k, sc, trk, own, theirs, fill, beside):
+        def place(t, n, counts, *toks):
+            return vec("ts", pou(t), n, counts[:, t % 2:t % 2 + 1], None, A.add, after=toks)
+
+        s0 = total(2 * f, H, 2 * H, cross(2 * f, k, H, [trk]))
+        b = cross(2 * f + 1, k, H)
+        v = fill[0](None)
         s1 = total(2 * k, 0, H, cross(2 * k, f, 0, [sc]))
+        v = fill[1](v)
+        b = halves(2 * f + 1, H, T.ce, 0, b)
         e = cross(2 * k + 1, f, 0)
-        beside()
+        beside(fill[2](v))
+        place(2 * f + 1, T.ce[:, 127:128], T.msg, b, *own)
+        place(2 * f, T.pl[:, 2 * f:2 * f + 1], T.msg, s0)
         e = halves(2 * k + 1, 0, T.cs, 0, e)
-        vec("copy", pou(2 * f, 2), T.pl[:, 2 * f:2 * f + 2], after=[s0])
-        vec("ts", pou(2 * k), T.pl[:, 2 * k:2 * k + 1], T.tms[:, 1:2], None, A.add, after=[s1, arrm])
-        return vec("ts", pou(2 * k + 1), T.cs[:, 127:128], T.tms[:, 2:3], None, A.add, after=[e])
+        place(2 * k, T.pl[:, 2 * k:2 * k + 1], T.tms, s1, theirs)
+        return place(2 * k + 1, T.cs[:, 127:128], T.tms, e)
 
-    def to_list(e, out, fill):
-        def step(*args, after=()):
-            e = vec(*args, after=after)
-            if fill:
-                fill.pop(0)()
-            return e
-
-        e = step("copy", T.win[:].indirect(T.pou[:]), T.val[:], after=[e, vval, vwin])
-        e = step("tr", T.wt[:], T.win[:, 0:256], after=[e])
+    def to_list(e, out):
+        e = vec("copy", T.win[:, 32:544].indirect(T.pou[:]), T.val[:], after=[e, vval, vwin])
+        vec("tr", T.wt[:, 0:256], T.win[:, 32:288], after=[e])
+        e = vec("tr", T.wt[:, 256:544], T.win[:, 16:304])
 
         def run(d, n, src, j):
-            return T.z[32 * d:32 * d + n, j:64:4], T.wt[32 * src:32 * src + n, 0:256:16]
+            return T.z[32 * d:32 * d + n, j:136:4], T.wt[32 * src:32 * src + n, 0:544:16]
 
         for d in range(4):
             s = act(*run(d, 32, d ^ 3, 3), F.Copy, after=[e])
@@ -201,26 +210,23 @@ def rank_program(g, core, T, topo):
         vec("copy", *run(2, 64, 0, 1))
         for d in range(3):
             e = vec("copy", *run(d, 32, d ^ 1, 2))
-        e = step("scan", T.zs[:], T.rz[:], T.z[:], 0.0, A.mult, A.add, after=[e, s, vrz])
-        e = vec("tr", T.gt[:], T.zs[:, 1:64:2], after=[e])
-        e = vec("copy", T.xt[:], T.gt[:].indirect(T.ud[:]), after=[e, vud])
-        e = vec("tr", T.xo[:], T.xt[:], after=[e])
-        vec("copy", out[:, 0:16:2], T.xo[:, 3:32:4], after=[e])
-        return vec("copy", out[:, 1:16:2], T.xo[:, 35:64:4])
+        e = vec("scan", T.zs[:], T.rz[:], T.z[:], 0.0, A.mult, A.add, after=[e, s, vrz])
+        return vec("ts", out[:], T.zs[:].indirect(T.fo[:, 0:1]), 256.0, None, A.add, after=[e, vfo])
 
     def pick(c_to, s_to, j, c, s, i0, i1, off, *toks):
         v = vec("copy", c_to[:, j:j + K].bitcast(dt.uint32), c[:, i0:i1].bitcast(dt.uint32).indirect(off[:]), after=toks)
         return v, act(s_to[:, j:j + K], s[:, i0:i1].indirect(off[:]), F.Copy, after=toks)
 
     vq = vec("quant", T.cx[:, 0:H], T.sx[:, 0:H], T.xb[:, 0:1024], after=[dx[0]])
-    tx, tr0 = score_half(T.cx, T.sx, 0, [vqu, vq])
+    tx, tr0 = score_half(T.cx, T.sx, 0, [vqu, vq], False)
     sc0 = column(0, tx)
     th0 = inside(0, sc0)
+    vfo, vrz, vval, vk16 = constants()
     vq = vec("quant", T.cx[:, H:2 * H], T.sx[:, H:2 * H], T.xb[:, 1024:2048], after=[dx[1]])
     own_half(0, sc0, th0, tr0)
-    tx, tr1 = score_half(T.cx, T.sx, 1, [vq])
+    tx, tr1 = score_half(T.cx, T.sx, 1, [vq], True)
     mylist = T[lst[rank]]
-    ql = to_list(places_first(0, 1, column(1, tx), tr1), mylist, [])
+    ql = to_list(places_first(0, 1, column(1, tx), tr1), mylist)
     p1 = pick(T.c1, T.s1, a0, T.cx, T.sx, 0, 512, mylist, ql)
 
     def send(c, s, j, to, arr, out, pk):
@@ -234,26 +240,30 @@ def rank_program(g, core, T, topo):
         return (arr, 2 * n), (out, 2 * n)
 
     arr1, out1 = send(T.c1, T.s1, a0, mate, "a1", "o1", p1)
-    tr, nl = [], 4
-    for i, r in enumerate(x for x in range(len(T.cores)) if x != rank):
+    tr, used, arrl = [], 0, {}
+    for r, n in ((mate, 8), (other, 4), (other ^ 1, 4)):
         rid, pid, _ = topo.addr(T.cores[r])
-        eng = topo.engines(core, T.cores[r])[nl * i:nl * i + nl]
+        eng = topo.engines(core, T.cores[r])[used:used + n]
+        used += n
         tr.append(RemoteDMATransfer(dst_ids=[DstId(rid=rid, pnc=pid)], dma_engine_mask=sum(1 << e for e in eng),
-                                    remote_sem=T.sem.al, src=mylist[:], dst=mylist[:]))
+                                    remote_sem=T.sem["al%d" % rank], src=mylist[:], dst=mylist[:]))
+        arrl[r] = ("al%d" % r, n)
     wait("g", ql)
     g.remote_dma_fused(tr, local_sem=T.sem.ol)
-    arrl, outl = ("al", nl * len(tr)), ("ol", nl * len(tr))
+    outl = ("ol", used)
 
     def columns(r):
-        return act(T.colr[:, 256 * r:256 * r + 256], T.iot[:].indirect(T[lst[r]][:]), F.Copy,
-                   after=[piot, ql if r == rank else arrl])
+        return act(T.colr[:, 256 * r:256 * r + 256], T.iot[:].indirect(T[lst[r]][:]), F.Identity, bias=512.0 * r,
+                   after=[piot, ql if r == rank else arrl[r]])
 
+    vkr = vec("ts", T.kr[:], T.k16[:], -1.0, 255.0, A.mult, A.add, after=[vk16])
+    vec("ts", T.k256[:], T.k16[:], -256.0, None, A.add)
     pr = pick(T.cr, T.sr, 0, T.c1, T.s1, a0, a0 + H, T.kr, vkr, *p1)
     t = mm(T.ps[:, 3072:3328], T.cu[:], T.su[:], T.cr[:], T.sr[:], after=pr)
     srv = act(T.rv[:], T.ps[:, 3072:3328], F.Copy, after=[t])
     vw = vec("quant", T.cw[:], T.sw[:], T.wb[:], after=[dw])
-    vwin = vec("set", T.win[:, 0:256], 0.0)
-    columns(rank)
+    vwin = vec("set", T.win[:, 0:304], 0.0)
+    spair = [columns(rank), columns(mate)]
 
     t = mm(T.ps[:, 3584:3840], T.cu[:], T.su[:], T.c1[:, b0:b0 + H], T.s1[:, b0:b0 + H], after=[arr1])
     rows = (T.rv[:], T.ps[:, 3584:3840]) if lower else (T.ps[:, 3584:3840], T.rv[:])
@@ -261,18 +271,27 @@ def rank_program(g, core, T, topo):
     mine = T.g1[:, 127:128]
     vm = vec("scan", T.g1[:], T.f1[:, 0:128], T.f1[:, 128:256], -256.0, A.add, A.add, after=[v])
 
-    def choice1(m, h1, *toks):
-        return vec("ts", h1[:], T.k256[:], m, m, A.is_ge, A.mult, after=toks)
+    def choice(m, h1, h2, out, tok):
+        return [lambda v: vec("ts", h1[:], T.k256[:], m, m, A.is_ge, A.mult, after=[tok]),
+                lambda v: vec("tt", h2[:], T.k16[:], h1[:], A.subtract, after=[v]),
+                lambda v: vec("copy", out[:], h2[:], after=[v])]
 
-    def choice2(h1, h2, *toks):
-        return vec("tt", h2[:], T.k16[:], h1[:], A.subtract, after=toks)
-
-    v = choice2(T.h1, T.h2, choice1(mine, T.h1, vm))
-    vc = vec("copy", T.q1[:], T.h2[:], after=[v])
+    vc = None
+    for step in choice(mine, T.h1, T.h2, T.q1, vm):
+        vc = step(vc)
     p2 = pick(T.c2, T.s2, H * f2, T.c1, T.s1, 0, 512, T.q1, vc, arr1, *p1)
-    vmsg = vec("copy", T.msg[:, 0:1], mine)
+    vmn = vec("copy", T.mn[:], mine)
 
     arr2, out2 = send(T.c2, T.s2, H * f2, other, "a2", "o2", p2)
+
+    def tell(src, dst, arr, out, *toks):
+        rid, pid, _ = topo.addr(T.cores[other])
+        m, n = topo.mask(core, T.cores[other]), len(topo.engines(core, T.cores[other]))
+        wait("g", *toks)
+        g.remote_dma(dst[:], src[:], T.sem[arr], T.sem[out], pid, rid, m)
+        return (arr, n), (out, n)
+
+    arrn, outn = tell(T.mn, T.tmn, "an", "on", vmn)
 
     def products(h, banks, toks):
         return [mm(T.ps[:, 512 * b:512 * b + H], T.cw[:, 128 * o:128 * o + 128], T.sw[:, 128 * o:128 * o + 128],
@@ -281,65 +300,50 @@ def rank_program(g, core, T, topo):
     def result(h, o, b):
         return T.yy[:, 512 * o + H * h:512 * o + H * h + H], T.ps[:, 512 * b:512 * b + H]
 
-    def who(h, m, n, *toks):
-        e = vec("ts", n[:], m, 256.0, None, A.add, after=toks)
-        return vec("ts", T.whow[:, H * h:H * h + H], T.iot[:, 0:H], n[:], 2.0 * h, A.is_ge, A.add, after=[piot, e])
-
     def col(h, lists, *toks):
         return act(T.colw[:, H * h:H * h + H], T.colr[:, 512 * h:512 * h + 512].indirect(lists[:]), F.Copy, after=toks)
 
-    tx, trf = score_half(T.c2, T.s2, f2, p2)
+    tx, trf = score_half(T.c2, T.s2, f2, p2, False)
     bf = [6, 7, 2 + 2 * k2, 3 + 2 * k2]
     typ = products(f2, bf, [vw])
     scf = column(f2, tx)
     thf = inside(f2, scf)
     d = own_half(f2, scf, thf, trf)
-    st = [total(2 * f2 + i, 0, H, d[i], T.msg[:, 1 + i:2 + i]) for i in (0, 1)]
-    wait("g", vmsg, *st)
-    rid, pid, _ = topo.addr(T.cores[other])
-    eng = topo.engines(core, T.cores[other])[0:4]
-    g.remote_dma(T.tms[:], T.msg[:], T.sem.am, T.sem.om, pid, rid, sum(1 << e for e in eng))
-    arrm, outm = ("am", len(eng)), ("om", len(eng))
-    for i in (0, 1):
-        act(T.fl[:, B * (2 * f2 + i) + 271:B * (2 * f2 + i) + 272], T.msg[:, 1 + i:2 + i], F.Copy, after=[st[i]])
+    st = [total(2 * f2 + i, 0, H, d[i], T.msg[:, i:i + 1]) for i in (0, 1)]
+    arrm, outm = tell(T.msg, T.tms, "am", "om", *st)
     done = [vec("copy", *result(f2, o, bf[o]), after=[typ[o]]) for o in range(O)]
-    who(f2, mine, T.part)
-    col(f2, T.q1, vc, columns(mate))
-    columns(other)
+    sother = [columns(other), columns(other ^ 1)]
+    sf = col(f2, T.q1, vc, *spair)
 
-    tx, trk = score_half(T.c2, T.s2, k2, [arr2, *done])
+    tx, trk = score_half(T.c2, T.s2, k2, [arr2], True, done)
     sck = column(k2, tx)
     bk = [6, 7, 2 + 2 * f2, 3 + 2 * f2]
     tyq = products(k2, bk, [scf, *thf])
-    last = {}
+    there, ids = [], []
 
-    def beside():
-        for o in range(3):
-            act(*result(k2, o, bk[o]), F.Copy, after=[tyq[o]])
+    def results(*os):
+        there.extend(act(*result(k2, o, bk[o]), F.Copy, after=[tyq[o]]) for o in os)
 
-    def fill1():
-        last["v"] = choice1(T.tms[:, 0:1], T.h3, arrm)
+    def beside(vq1o):
+        results(0, 1)
+        ids.append(col(k2, T.q1o, vq1o, *sother))
 
-    def fill2():
-        last["v"] = choice2(T.h3, T.h4, last["v"])
+    fill = choice(T.tmn[:], T.h3, T.h4, T.q1o, arrn)
+    v2 = to_list(places_last(f2, k2, sck, trk, st, arrm, fill, beside), T.q2)
+    results(2, 3)
 
-    def fill3():
-        last["v"] = vec("copy", T.q1o[:], T.h4[:], after=[last["v"]])
-
-    v2 = to_list(places_last(f2, k2, sck, trk, arrm, beside), T.q2, [fill1, fill2, fill3])
-    sy = act(*result(k2, 3, bk[3]), F.Copy, after=[tyq[3]])
-    sid = col(k2, T.q1o, columns(other ^ 1), last["v"])
-
+    vsel = vec("ts", T.sel[:], T.zs[:].indirect(T.fi[:, 0:1]), 256.0, None, A.add)
     for o in range(O):
         src, out = T.yy[:, 512 * o:512 * o + 512].indirect(T.q2[:]), T.ysb[:, K * o:K * o + K]
-        toks = [v2, *done, sy]
+        toks = [v2, done[o], there[o]]
         wait("y", vec("copy", out, src, after=toks) if o % 2 == 0 else act(out, src, F.Copy, after=toks))
         inc("dy", g.sync.dma_start(T.y[:, K * o:K * o + K], out), 16)
-    v = vec("copy", T.wo[:], T.whow[:].indirect(T.q2[:]), after=[who(k2, T.tms[:, 0:1], T.npart)])
-    s = act(T.co[:], T.colw[:].indirect(T.q2[:]), F.Copy, after=[sid])
-    wait("y", s)
-    inc("did", g.sync.dma_start(T.id[1:2, :], T.co[0:1, :]), 16)
-    wait("y", v)
-    inc("did", g.sync.dma_start(T.id[0:1, :], T.wo[0:1, :]), 16)
+        if o == 0:
+            v = vec("copy", T.idi[:], T.colw[:].indirect(T.sel[:, 0:2]), after=[vsel, sf, *ids])
+    vec("ts", T.idv[:, 0:32], T.idi[:], 9, None, A.arith_shift_right, after=[v])
+    v = vec("ts", T.idv[:, 32:64], T.idi[:], 511, None, A.bitwise_and)
+    wait("y", vec("copy", T.idf[:], T.idv[:], after=[v]))
+    for i in (0, 1):
+        inc("did", g.sync.dma_start(T.id[i:i + 1, :], T.idf[0:128:16, 32 * i:32 * i + 32]), 16)
 
-    wait("g", out1, outl, out2, outm, arr1, arrl, arr2, arrm, *[(s, n) for s, n in cnt.items()])
+    wait("g", out1, outl, out2, outn, outm, arr1, *arrl.values(), arr2, arrn, arrm, *[(s, n) for s, n in cnt.items()])

@@ -11,16 +11,18 @@ def _bufs(dtype, **widths):
         SCRATCH[name] = ("sbuf", [128, n], dtype)
 
 
-_bufs("float8_e4m3fn_x4", cx=512, cu=128, cw=512, c1=512, cr=256, c2=512)
-_bufs("uint8", sx=512, su=128, sw=512, s1=512, sr=256, s2=512)
-_bufs("bfloat16", xb=2048, wb=2048, ub=16, up=512, neg=128, dm=128, fl=2048, cs=256, ce=256, f1=256, g1=128,
-      val=64, win=544, wt=544, z=136, zs=136, rz=136)
-_bufs("float32", sc4=4, nd=4, th=512, pl=4, vb=64, hc=1, fx=1, fy=1, fz=1, fw=1, k16=16, k256=16, iot=512, rv=256,
-      h1=16, h2=16, h3=16, h4=16, mn=1, tmn=1, msg=2, tms=2, colr=1024, colw=512, idf=64, yy=2048, ysb=1024)
-_bufs("int32", ip=32, i3=32, i15=16, c16=16, ri=136, y17=1, a14=1, a112=1, idi=32, idv=64)
-_bufs("uint16", u4=32, pou=4, kr=16, fo=2, fi=2, sel=16, l0=16, l1=16, l2=16, l3=16, q1=16, q1o=16, q2=16)
-SEMAPHORES = ["cv", "ca", "ct", "cp", "du", "dx0", "dx1", "dw", "dy", "did",
-              "a1", "o1", "al0", "al1", "al2", "al3", "ol", "a2", "o2", "an", "on", "am", "om"]
+_bufs("float8_e4m3fn_x4", cx=512, cu=128, cw=512, c1=512, c2=512)
+_bufs("uint8", sx=512, su=128, sw=512, s1=512, s2=512)
+_bufs("bfloat16", xb=2048, wb=2048, ub=16, up=512, neg=128, dm=128, fl=2048, cs=256, ce=512, f1=256, g1=128,
+      val=64, win=800, wt=544, z=136, zs=136, rz=136, iot=256, rep=1024, colr=1024, whow=512,
+      m0=6, m1=6, m2=6, m3=6, n0=16, n1=16, n2=16, n3=16)
+_bufs("float32", sc4=4, nd=4, th=512, pl=4, vb=64, hc=1, fx=1, fy=1, fz=1, fw=1, k16=16, k256=16, kb=2, rv=256,
+      h1=16, h2=16, h3=16, h4=16, k0=2, k1=2, k2=2, k3=2, sel=2, cp=1, t1=4, t2=4, t3=4,
+      cc=1, colw=512, idf=64, yy=2048, ysb=1024)
+_bufs("int32", ip=32, i3=32, i15=16, c16=16, c2i=16, ri=136, y17=1, a14=1, a112=1)
+_bufs("uint16", u4=32, pou=4, fo=2, fi=2, isl=16, r32=16, lst=16, q1=16, q1o=16, q2=16)
+SEMAPHORES = ["cv", "ca", "ct", "cp", "du", "dx0", "dx1", "dw", "dy0", "dy1", "did", "a1", "o1", "a2", "o2", "on", "ok", "om",
+              "an0", "an1", "an2", "an3", "ak0", "ak1", "ak2", "ak3", "am0", "am1", "am2", "am3"]
 STEP, TINY = 1.125 * 2.0 ** -24, 2.0 ** -124
 
 
@@ -61,13 +63,13 @@ def rank_program(g, core, T, topo):
         wait("t", *after)
         return inc("ct", g.tensor.matmul_mx(out, a, sa, b, sb, True, True))
 
-    lst = ["l0", "l1", "l2", "l3"]
     mate, other = rank ^ 1, rank ^ 2
     lower = rank < mate
     a0 = 0 if lower else H
     b0 = H - a0
     f2 = 0 if rank < other else 1
     k2 = 1 - f2
+    blk = 0 if lower else 1
 
     du = inc("du", g.scalar.dma_start(T.ub[:, 0:4], T.u[:, 0:4]), 16)
     dx = [inc("dx%d" % h, g.sync.dma_start(T.xb[:, 1024 * h:1024 * h + 1024], T.x[:, 1024 * h:1024 * h + 1024]), 16)
@@ -78,20 +80,23 @@ def rank_program(g, core, T, topo):
     f = {"allow_small_or_imprecise_dtypes": True}
     pip = inc("cp", g.iota(T.ip[:], [[0, 32]], 0, 1))
     wait("g", vneg)
-    pdm = inc("cp", g.affine_select(T.dm[:], T.neg[:], [[-1, 128]], A.is_gt, 0.0, 0, 1))
+    pdm = inc("cp", g.affine_select(T.dm[:], T.neg[:], [[-1, 128]], A.is_gt if lower else A.is_ge, 0.0, 0, 1))
     pri = inc("cp", g.iota(T.ri[:], [[0, 17], [1, 8]], 0, 0))
     pvb = inc("cp", g.iota(T.vb[:], [[128, 4], [1, 16]], 0, 0, **f))
     pc16 = inc("cp", g.iota(T.c16[:], [[16, 16]], 0, 0))
-    piot = inc("cp", g.iota(T.iot[:], [[1, 512]], 0, 0, **f))
+    pc2 = inc("cp", g.iota(T.c2i[:], [[1, 8], [0, 2]], 0, 0))
+    piot = inc("cp", g.iota(T.iot[:], [[1, 256]], -256, 0, **f))
+    pkb = inc("cp", g.iota(T.kb[:], [[128 if lower else -128, 2]], -256 if lower else -1, 1 if lower else -1, **f))
     v = vec("ts", T.i3[:], T.ip[:], 3, None, A.bitwise_and, after=[pip])
+    vu4 = vec("copy", T.u4[:], T.i3[:], after=[v])
     v15 = vec("ts", T.i15[:], T.ip[:, 0:16], 15, None, A.bitwise_and)
     for out, bits in ((T.y17, 17), (T.a14, 14), (T.a112, 112)):
         va = vec("ts", out[:], T.ip[:, 0:1], bits, None, A.bitwise_and)
-    vu4 = vec("copy", T.u4[:], T.i3[:], after=[v])
+    w0 = 32 if lower else 32 + H
+    vwin = vec("set", T.win[:, w0 - 16:w0 + 272], 0.0)
     s = act(T.up[:, 256:512], T.ub[:, 0:4].indirect(T.u4[:, 16:32]), F.Copy, after=[du, vu4])
     v = vec("copy", T.up[:, 0:256], T.ub[:, 0:4].indirect(T.u4[:, 0:16]), after=[du, vu4])
     vqu = vec("quant", T.cu[:], T.su[:], T.up[:], after=[v, s])
-    vwin = vec("set", T.win[:, 0:304], 0.0)
     vec("tt", T.hc[:], T.ip[:, 0:1], T.i15[:, 0:1], A.subtract, after=[v15])
     vec("ts", T.fx[:], T.y17[:], 1, 72.0, A.is_equal, A.mult, after=[va])
     vec("ts", T.fy[:], T.y17[:], 16, 64.0, A.is_equal, A.mult)
@@ -103,19 +108,17 @@ def rank_program(g, core, T, topo):
         vfo = vec("ts", T.fi[:, 0:1], T.fx[:], T.fy[:], T.fw[:], A.add, A.add)
         vrz = vec("ts", T.rz[:], T.ri[:], 0, None, A.is_gt, after=[pri])
         vval = vec("ts", T.val[:], T.vb[:], T.hc[:], -256.0, A.add, A.add, after=[pvb, vf])
-        vk16 = vec("tt", T.k16[:], T.i15[:], T.c16[:], A.add, after=[pc16])
-        return vfo, vrz, vval, vk16
+        return vfo, vrz, vval
 
-    def score_half(c, s, h, toks, row_first, later=()):
+    def score_half(h, toks, row_first):
         def row():
-            return mm(T.ps[:, 512 * h:512 * h + H], T.cu[:], T.su[:], c[:, H * h:H * h + H], s[:, H * h:H * h + H])
+            return mm(T.ps[:, 512 * h:512 * h + H], T.cu[:], T.su[:], T.cx[:, H * h:H * h + H], T.sx[:, H * h:H * h + H])
 
         wait("t", *toks)
         r = row() if row_first else None
-        wait("t", *later)
         for t in (2 * h, 2 * h + 1):
-            x = mm(T.ps[:, 512 * (2 + t):512 * (2 + t) + 128], c[:, 128 * t:128 * t + 128], s[:, 128 * t:128 * t + 128],
-                   T.cu[:], T.su[:])
+            x = mm(T.ps[:, 512 * (2 + t):512 * (2 + t) + 128], T.cx[:, 128 * t:128 * t + 128],
+                   T.sx[:, 128 * t:128 * t + 128], T.cu[:], T.su[:])
         return x, r or row()
 
     def column(h, tx):
@@ -128,106 +131,77 @@ def rank_program(g, core, T, topo):
 
     def plain(t, j0, j1, at, toks=()):
         p = 512 * (j0 // H) + j0 % H
+        if j1 <= 128 * t:
+            op = A.is_ge if lower else A.is_lt
+        else:
+            op = A.is_gt if lower else A.is_le
         return vec("ts", T.fl[:, 512 * t + at:512 * t + at + j1 - j0], T.ps[:, p:p + j1 - j0], T.sc4[:, t:t + 1], None,
-                   A.is_ge if j1 <= 128 * t else A.is_gt, after=toks)
+                   op, after=toks)
 
     def diag(t, at, tok):
         p = 512 * (t // 2) + 128 * (t % 2)
         return vec("tt", T.fl[:, 512 * t + at:512 * t + at + 128], T.ps[:, p:p + 128], T.th[:, 128 * t:128 * t + 128],
-                   A.is_gt, after=[tok])
+                   A.is_gt if lower else A.is_le, after=[tok])
 
-    def total(t, i0, i1, tok, out=None):
+    def total(t, i0, i1, tok):
         fl = T.fl[:, 512 * t + i0:512 * t + i1]
-        return act(fl, fl, F.Copy, after=[tok], accum_out=T.pl[:, t:t + 1] if out is None else out)
+        return act(fl, fl, F.Copy, after=[tok], accum_out=T.pl[:, t:t + 1])
 
-    def halves(t, i, cs, j, tok):
-        z = 512 * t + i
+    def halves(z, cs, j, tok):
         return vec("scan", cs[:, j:j + 128], T.fl[:, z:z + 128], T.fl[:, z + 128:z + 256], 0.0, A.add, A.add, after=[tok])
 
-    def own_half(h, sc, th, tr):
-        plain(2 * h, H * h + 128, H * h + 256, 128, [sc, tr])
-        plain(2 * h + 1, H * h, H * h + 128, 0)
-        return diag(2 * h, 0, th[0]), diag(2 * h + 1, 128, th[1])
+    def row_sum(t, tok):
+        z, j = 512 * t, 256 * (t // 2)
+        return vec("scan", T.ce[:, j:j + 256], T.fl[:, z:z + 256], T.fl[:, z + 256:z + 512], -256.0, A.add, A.add, after=[tok])
 
     def cross(t, h, at, toks=()):
         return plain(t, H * h, H * h + H, at, toks)
 
-    def pou(t, n=1):
-        return T.pou[:, t:t + n]
-
-    def places_first(f, k, sc, trk):
+    def places(f, k, sc, trk):
         a = cross(2 * f, k, H, [trk])
         b = cross(2 * f + 1, k, H)
         th = inside(k, sc)
         s0 = total(2 * f, 0, 512, a)
         cross(2 * k, f, 0, [sc])
-        halves(2 * f + 1, 0, T.ce, 0, b)
-        b = halves(2 * f + 1, H, T.ce, 128, b)
+        row_sum(2 * f + 1, b)
         plain(2 * k, H * k + 128, H * k + 256, H + 128)
         s1 = total(2 * k, 0, 512, diag(2 * k, H, th[0]))
         t = 2 * k + 1
-        c = cross(t, f, 0)
+        cross(t, f, 0)
         plain(t, H * k, H * k + 128, H)
-        halves(t, 0, T.cs, 0, c)
-        e = diag(t, H + 128, th[1])
-        vec("ts", pou(2 * f + 1), T.ce[:, 127:128], T.ce[:, 255:256], None, A.add, after=[b])
-        vec("copy", pou(2 * f), T.pl[:, 2 * f:2 * f + 1], after=[s0])
-        e = halves(t, H, T.cs, 128, e)
-        vec("copy", pou(2 * k), T.pl[:, 2 * k:2 * k + 1], after=[s1])
-        return vec("ts", pou(t), T.cs[:, 127:128], T.cs[:, 255:256], None, A.add, after=[e])
+        e = row_sum(t, diag(t, H + 128, th[1]))
+        vec("ts", T.pou[:, 1:4:2], T.ce[:, 255:512:256], 256.0, None, A.add, after=[e])
+        return vec("copy", T.pou[:, 0:4:2], T.pl[:, 0:4:2], after=[s0, s1])
 
-    def places_last(f, k, sc, trk, own, theirs, fill, beside):
-        def place(t, n, counts, *toks):
-            return vec("ts", pou(t), n, counts[:, t % 2:t % 2 + 1], None, A.add, after=toks)
-
-        s0 = total(2 * f, H, 2 * H, cross(2 * f, k, H, [trk]))
-        b = cross(2 * f + 1, k, H)
-        v = fill[0](None)
-        s1 = total(2 * k, 0, H, cross(2 * k, f, 0, [sc]))
-        v = fill[1](v)
-        b = halves(2 * f + 1, H, T.ce, 0, b)
-        e = cross(2 * k + 1, f, 0)
-        beside(fill[2](v))
-        place(2 * f + 1, T.ce[:, 127:128], T.msg, b, *own)
-        place(2 * f, T.pl[:, 2 * f:2 * f + 1], T.msg, s0)
-        e = halves(2 * k + 1, 0, T.cs, 0, e)
-        place(2 * k, T.pl[:, 2 * k:2 * k + 1], T.tms, s1, theirs)
-        return place(2 * k + 1, T.cs[:, 127:128], T.tms, e)
-
-    def to_list(e, out):
-        e = vec("copy", T.win[:, 32:544].indirect(T.pou[:]), T.val[:], after=[e, vval, vwin])
-        vec("tr", T.wt[:, 0:256], T.win[:, 32:288], after=[e])
-        e = vec("tr", T.wt[:, 256:544], T.win[:, 16:304])
-
-        def run(d, n, src, j):
-            return T.z[32 * d:32 * d + n, j:136:4], T.wt[32 * src:32 * src + n, 0:544:16]
-
-        for d in range(4):
-            s = act(*run(d, 32, d ^ 3, 3), F.Copy, after=[e])
-        s = act(*run(3, 32, 2, 2), F.Copy)
-        vec("copy", *run(0, 128, 0, 0), after=[e])
-        vec("copy", *run(0, 64, 2, 1))
-        vec("copy", *run(2, 64, 0, 1))
-        for d in range(3):
-            e = vec("copy", *run(d, 32, d ^ 1, 2))
-        e = vec("scan", T.zs[:], T.rz[:], T.z[:], 0.0, A.mult, A.add, after=[e, s, vrz])
-        return vec("ts", out[:], T.zs[:].indirect(T.fo[:, 0:1]), 256.0, None, A.add, after=[e, vfo])
+    def to_list(e, out, w0, w1, n):
+        e = vec("copy", T.win[:, 32:w1].indirect(T.pou[:]), T.val[:], after=[e, vval, vwin])
+        vec("tr", T.wt[:, 0:256], T.win[:, w0:w0 + 256], after=[e])
+        e = vec("tr", T.wt[:, 256:544], T.win[:, w0 - 16:w0 + 272])
+        runs = [(0, 128, 0, 0), (0, 64, 2, 1), (2, 64, 0, 1), *[(d, 32, d ^ 1, 2) for d in range(4)],
+                *[(d, 32, d ^ 3, 3) for d in range(4)]]
+        toks = []
+        for i, (d, m, src, j) in enumerate(runs):
+            ab = T.z[32 * d:32 * d + m, j:136:4], T.wt[32 * src:32 * src + m, 0:544:16]
+            toks.append(vec("copy", *ab, after=[e]) if i < 11 - n else act(*ab, F.Copy, after=[e]))
+        e = vec("scan", T.zs[:], T.rz[:], T.z[:], 0.0, A.mult, A.add, after=[*toks, vrz])
+        return e, vec("ts", out[:], T.zs[:].indirect(T.fo[:, 0:1]), 256.0, None, A.add, after=[e, vfo])
 
     def pick(c_to, s_to, j, c, s, i0, i1, off, *toks):
         v = vec("copy", c_to[:, j:j + K].bitcast(dt.uint32), c[:, i0:i1].bitcast(dt.uint32).indirect(off[:]), after=toks)
         return v, act(s_to[:, j:j + K], s[:, i0:i1].indirect(off[:]), F.Copy, after=toks)
 
     vq = vec("quant", T.cx[:, 0:H], T.sx[:, 0:H], T.xb[:, 0:1024], after=[dx[0]])
-    tx, tr0 = score_half(T.cx, T.sx, 0, [vqu, vq], False)
+    tx, tr0 = score_half(0, [vqu, vq], False)
     sc0 = column(0, tx)
     th0 = inside(0, sc0)
-    vfo, vrz, vval, vk16 = constants()
+    vfo, vrz, vval = constants()
     vq = vec("quant", T.cx[:, H:2 * H], T.sx[:, H:2 * H], T.xb[:, 1024:2048], after=[dx[1]])
-    own_half(0, sc0, th0, tr0)
-    tx, tr1 = score_half(T.cx, T.sx, 1, [vq], True)
-    mylist = T[lst[rank]]
-    ql = to_list(places_first(0, 1, column(1, tx), tr1), mylist)
-    p1 = pick(T.c1, T.s1, a0, T.cx, T.sx, 0, 512, mylist, ql)
+    plain(0, 128, 256, 128, [sc0, tr0])
+    plain(1, 0, 128, 0)
+    diag(0, 0, th0[0])
+    diag(1, 128, th0[1])
+    tx, tr1 = score_half(1, [vq], True)
+    zl, ql = to_list(places(0, 1, column(1, tx), tr1), T.lst, w0, 544, 5)
 
     def send(c, s, j, to, arr, out, pk):
         rid, pid, _ = topo.addr(T.cores[to])
@@ -239,59 +213,93 @@ def rank_program(g, core, T, topo):
         g.remote_dma(s[:, j:j + K], s[:, j:j + K], T.sem[arr], T.sem[out], pid, rid, m)
         return (arr, 2 * n), (out, 2 * n)
 
+    def tell(what, n, *toks):
+        tr, arr = [], {}
+        for i, r in enumerate((mate, other, other ^ 1)):
+            rid, pid, _ = topo.addr(T.cores[r])
+            eng = topo.engines(core, T.cores[r])[4 * i:4 * i + 4]
+            me = T["%s%d" % (what, rank)][:, 0:n]
+            tr.append(RemoteDMATransfer(dst_ids=[DstId(rid=rid, pnc=pid)], dma_engine_mask=sum(1 << e for e in eng),
+                                        remote_sem=T.sem["a%s%d" % (what, rank)], src=me, dst=me))
+            arr[r] = ("a%s%d" % (what, r), 4)
+        wait("g", *toks)
+        g.remote_dma_fused(tr, local_sem=T.sem["o" + what])
+        return arr, ("o" + what, 12)
+
+    snum = act(T["n%d" % rank][:, 0:8], T.zs[:, 7:64:8], F.Copy, after=[zl])
+    arrn, outn = tell("n", 8, snum)
+    p1 = pick(T.c1, T.s1, a0, T.cx, T.sx, 0, 512, T.lst, ql)
     arr1, out1 = send(T.c1, T.s1, a0, mate, "a1", "o1", p1)
-    tr, used, arrl = [], 0, {}
-    for r, n in ((mate, 8), (other, 4), (other ^ 1, 4)):
-        rid, pid, _ = topo.addr(T.cores[r])
-        eng = topo.engines(core, T.cores[r])[used:used + n]
-        used += n
-        tr.append(RemoteDMATransfer(dst_ids=[DstId(rid=rid, pnc=pid)], dma_engine_mask=sum(1 << e for e in eng),
-                                    remote_sem=T.sem["al%d" % rank], src=mylist[:], dst=mylist[:]))
-        arrl[r] = ("al%d" % r, n)
-    wait("g", ql)
-    g.remote_dma_fused(tr, local_sem=T.sem.ol)
-    outl = ("ol", used)
+    wait("t", *p1)
+    for t in (0, 1):
+        tx = mm(T.ps[:, 512 * (2 + t):512 * (2 + t) + 128], T.c1[:, a0 + 128 * t:a0 + 128 * t + 128],
+                T.s1[:, a0 + 128 * t:a0 + 128 * t + 128], T.cu[:], T.su[:])
+    sk = act(T["k%d" % rank][:, 0:2], T.ps[:, 1024:2048:512], F.Copy, after=[tx])
+    arrk, outk = tell("k", 2, sk)
 
-    def columns(r):
-        return act(T.colr[:, 256 * r:256 * r + 256], T.iot[:].indirect(T[lst[r]][:]), F.Identity, bias=512.0 * r,
-                   after=[piot, ql if r == rank else arrl[r]])
-
-    vkr = vec("ts", T.kr[:], T.k16[:], -1.0, 255.0, A.mult, A.add, after=[vk16])
-    vec("ts", T.k256[:], T.k16[:], -256.0, None, A.add)
-    pr = pick(T.cr, T.sr, 0, T.c1, T.s1, a0, a0 + H, T.kr, vkr, *p1)
-    t = mm(T.ps[:, 3072:3328], T.cu[:], T.su[:], T.cr[:], T.sr[:], after=pr)
-    srv = act(T.rv[:], T.ps[:, 3072:3328], F.Copy, after=[t])
+    vr32 = vec("copy", T.r32[:], T.c2i[:], after=[pc2])
+    vk16 = vec("tt", T.k16[:], T.i15[:], T.c16[:], A.add, after=[pc16])
+    vec("ts", T.k256[:], T.k16[:], -256.0, None, A.add, after=[vk16])
+    vm = vec("set", T["m%d" % rank][:], 0.0)
     vw = vec("quant", T.cw[:], T.sw[:], T.wb[:], after=[dw])
-    vwin = vec("set", T.win[:, 0:304], 0.0)
-    spair = [columns(rank), columns(mate)]
+    vwin = vec("set", T.win[:, 16:304], 0.0)
 
-    t = mm(T.ps[:, 3584:3840], T.cu[:], T.su[:], T.c1[:, b0:b0 + H], T.s1[:, b0:b0 + H], after=[arr1])
-    rows = (T.rv[:], T.ps[:, 3584:3840]) if lower else (T.ps[:, 3584:3840], T.rv[:])
-    v = vec("tt", T.f1[:], rows[0], rows[1], A.is_ge, after=[t, srv])
+    def replicated(r):
+        return act(T.rep[:, 256 * r:256 * r + 256], T["n%d" % r][:, 0:8].indirect(T.r32[:]), F.Copy,
+                   after=[vr32, snum if r == rank else arrn[r]])
+
+    def turned(r, tok):
+        return vec("tr", T.colr[:, 256 * r:256 * r + 256], T.rep[:, 256 * r:256 * r + 256], after=[tok])
+
+    rp = {rank: replicated(rank)}
+    t = mm(T.ps[:, 0:256], T.cu[:], T.su[:], T.c1[:, a0:a0 + H], T.s1[:, a0:a0 + H])
+    srv = act(T.rv[:], T.ps[:, 0:256], F.Copy, after=[t])
+    for r in (mate, other):
+        rp[r] = replicated(r)
+    tu = {r: turned(r, rp[r]) for r in (rank, mate)}
+
+    def kk(r, t, n=1):
+        return T["k%d" % r][:, t:t + n]
+
+    vcp = vec("tt", T.cp[:], kk(other, blk), kk(other ^ 1, blk), A.max, after=[arrk[other], arrk[other ^ 1]])
+    vsel = vec("tt", T.sel[:], kk(rank, 0, 2), kk(mate, 0, 2), A.is_ge if lower else A.is_gt, after=[arrk[mate], sk])
+
+    def sides(at, row, *toks):
+        return act(T.fl[:, at:at + H], row, F.Sign, scale=-1.0, bias=T.cp[:], after=[vcp, *toks])
+
+    sides(0, T.rv[:], srv)
+
+    row = [mm(T.ps[:, b:b + H], T.cu[:], T.su[:], T.c1[:, b0:b0 + H], T.s1[:, b0:b0 + H], after=[arr1, sk]) for b in (512, 1024)]
+    theirs = T.ps[:, 512:768]
+    rows = (T.rv[:], theirs) if lower else (theirs, T.rv[:])
+    v = vec("tt", T.f1[:], rows[0], rows[1], A.is_ge, after=[row[0], srv])
     mine = T.g1[:, 127:128]
-    vm = vec("scan", T.g1[:], T.f1[:, 0:128], T.f1[:, 128:256], -256.0, A.add, A.add, after=[v])
+    vm1 = vec("scan", T.g1[:], T.f1[:, 0:128], T.f1[:, 128:256], -256.0, A.add, A.add, after=[v])
 
-    def choice(m, h1, h2, out, tok):
-        return [lambda v: vec("ts", h1[:], T.k256[:], m, m, A.is_ge, A.mult, after=[tok]),
-                lambda v: vec("tt", h2[:], T.k16[:], h1[:], A.subtract, after=[v]),
-                lambda v: vec("copy", out[:], h2[:], after=[v])]
+    def choice(m, h1, h2, out, *toks):
+        v = vec("ts", h1[:], T.k256[:], m, 256.0, A.is_ge, A.mult, after=toks)
+        v = vec("tt", h2[:], T.k16[:], h1[:], A.add, after=[v])
+        return vec("copy", out[:], h2[:], after=[v])
 
-    vc = None
-    for step in choice(mine, T.h1, T.h2, T.q1, vm):
-        vc = step(vc)
+    vc = choice(mine, T.h1, T.h2, T.q1, vm1)
+    ss = sides(H, T.ps[:, 1024:1280], row[1])
     p2 = pick(T.c2, T.s2, H * f2, T.c1, T.s1, 0, 512, T.q1, vc, arr1, *p1)
-    vmn = vec("copy", T.mn[:], mine)
 
     arr2, out2 = send(T.c2, T.s2, H * f2, other, "a2", "o2", p2)
 
-    def tell(src, dst, arr, out, *toks):
-        rid, pid, _ = topo.addr(T.cores[other])
-        m, n = topo.mask(core, T.cores[other]), len(topo.engines(core, T.cores[other]))
-        wait("g", *toks)
-        g.remote_dma(dst[:], src[:], T.sem[arr], T.sem[out], pid, rid, m)
-        return (arr, n), (out, n)
-
-    arrn, outn = tell(T.mn, T.tmn, "an", "on", vmn)
+    msg = T["m%d" % rank]
+    sc = act(T.fl[:, 512:1024], T.fl[:, 0:512], F.Relu, scale=1.0 if f2 == 0 else -1.0, accum_out=T.cc[:], after=[ss])
+    smine = act(msg[:, 4:5], mine, F.Copy, after=[vm1, vm])
+    c = [vec("ts", T.fl[:, 1024 + H * i:1280 + H * i], theirs, kk(rank, i), None, A.is_gt if lower else A.is_ge)
+         for i in (0, 1)]
+    c = [halves(1024 + H * i, T.cs, 128 * i, c[i]) for i in (0, 1)]
+    for i in (0, 1):
+        at = 2 * f2 + i
+        vec("ts", msg[:, at:at + 1], T.cs[:, 128 * i + 127:128 * i + 128], T.kb[:, i:i + 1], T.sel[:, i:i + 1],
+            A.add, A.mult, after=[c[i], pkb, vsel, vm])
+    at, sign = 2 * k2 + blk, -1.0 if f2 == 0 else 1.0
+    vmsg = vec("ts", msg[:, at:at + 1], T.cc[:], sign, -256.0 * sign, A.mult, A.add, after=[sc])
+    arrm, outm = tell("m", 6, vmsg, smine)
 
     def products(h, banks, toks):
         return [mm(T.ps[:, 512 * b:512 * b + H], T.cw[:, 128 * o:128 * o + 128], T.sw[:, 128 * o:128 * o + 128],
@@ -301,49 +309,56 @@ def rank_program(g, core, T, topo):
         return T.yy[:, 512 * o + H * h:512 * o + H * h + H], T.ps[:, 512 * b:512 * b + H]
 
     def col(h, lists, *toks):
-        return act(T.colw[:, H * h:H * h + H], T.colr[:, 512 * h:512 * h + 512].indirect(lists[:]), F.Copy, after=toks)
+        return act(T.colw[:, H * h:H * h + H], T.colr[:, 512 * h:512 * h + 512].indirect(lists[:]), F.Identity, bias=256.0,
+                   after=toks)
 
-    tx, trf = score_half(T.c2, T.s2, f2, p2, False)
-    bf = [6, 7, 2 + 2 * k2, 3 + 2 * k2]
-    typ = products(f2, bf, [vw])
-    scf = column(f2, tx)
-    thf = inside(f2, scf)
-    d = own_half(f2, scf, thf, trf)
-    st = [total(2 * f2 + i, 0, H, d[i], T.msg[:, i:i + 1]) for i in (0, 1)]
-    arrm, outm = tell(T.msg, T.tms, "am", "om", *st)
-    done = [vec("copy", *result(f2, o, bf[o]), after=[typ[o]]) for o in range(O)]
-    sother = [columns(other), columns(other ^ 1)]
-    sf = col(f2, T.q1, vc, *spair)
+    def who(h, m, *toks):
+        return vec("ts", T.whow[:, H * h:H * h + H], T.iot[:], m, 2.0 * h, A.is_ge, A.add, after=[piot, *toks])
 
-    tx, trk = score_half(T.c2, T.s2, k2, [arr2], True, done)
-    sck = column(k2, tx)
-    bk = [6, 7, 2 + 2 * f2, 3 + 2 * f2]
-    tyq = products(k2, bk, [scf, *thf])
-    there, ids = [], []
+    bf, bk = [4, 5, 6, 7], [2, 3, 0, 1]
+    typ = products(f2, bf, [vw, *p2])
+    vf = who(f2, mine)
+    tu[other] = turned(other, rp[other])
+    done = [act(*result(f2, o, bf[o]), F.Copy, after=[typ[o]]) for o in (0, 1)]
+    rp[other ^ 1] = replicated(other ^ 1)
+    done += [vec("copy", *result(f2, o, bf[o]), after=[typ[o]]) for o in (2, 3)]
+    tu[other ^ 1] = turned(other ^ 1, rp[other ^ 1])
+    sf = col(f2, T.q1, vc, tu[rank], tu[mate])
+    tyq = products(k2, bk, [arr2, sk, srv, vmsg, ss])
+
+    def m4(r):
+        return T["m%d" % r][:, 0:4]
 
     def results(*os):
-        there.extend(act(*result(k2, o, bk[o]), F.Copy, after=[tyq[o]]) for o in os)
+        return [act(*result(k2, o, bk[o]), F.Copy, after=[tyq[o]]) for o in os]
 
-    def beside(vq1o):
-        results(0, 1)
-        ids.append(col(k2, T.q1o, vq1o, *sother))
+    there = results(0, 1)
+    v = vec("tt", T.t1[:], m4(rank), m4(mate), A.add, after=[vmsg, arrm[mate]])
+    v = vec("tt", T.t2[:], T.t1[:], m4(other), A.add, after=[v, arrm[other]])
+    v = vec("tt", T.t3[:], T.t2[:], m4(other ^ 1), A.add, after=[v, arrm[other ^ 1]])
+    v = vec("ts", T.pou[:], T.t3[:], 512.0, None, A.add, after=[v])
+    v2 = to_list(v, T.q2, 32, 800, 3)[1]
+    there += results(2, 3)
 
-    fill = choice(T.tmn[:], T.h3, T.h4, T.q1o, arrn)
-    v2 = to_list(places_last(f2, k2, sck, trk, st, arrm, fill, beside), T.q2)
-    results(2, 3)
-
-    vsel = vec("ts", T.sel[:], T.zs[:].indirect(T.fi[:, 0:1]), 256.0, None, A.add)
+    mo = T["m%d" % other][:, 4:5]
     for o in range(O):
         src, out = T.yy[:, 512 * o:512 * o + 512].indirect(T.q2[:]), T.ysb[:, K * o:K * o + K]
         toks = [v2, done[o], there[o]]
-        wait("y", vec("copy", out, src, after=toks) if o % 2 == 0 else act(out, src, F.Copy, after=toks))
-        inc("dy", g.sync.dma_start(T.y[:, K * o:K * o + K], out), 16)
+        tok = vec("copy", out, src, after=toks) if o % 2 == 0 else act(out, src, F.Copy, after=toks)
+        y = "s" if o == 3 else "y"
+        wait(y, tok)
+        inc("dy%d" % (o == 3), q[y].dma_start(T.y[:, K * o:K * o + K], out), 16)
         if o == 0:
-            v = vec("copy", T.idi[:], T.colw[:].indirect(T.sel[:, 0:2]), after=[vsel, sf, *ids])
-    vec("ts", T.idv[:, 0:32], T.idi[:], 9, None, A.arith_shift_right, after=[v])
-    v = vec("ts", T.idv[:, 32:64], T.idi[:], 511, None, A.bitwise_and)
-    wait("y", vec("copy", T.idf[:], T.idv[:], after=[v]))
+            vo = choice(mo, T.h3, T.h4, T.q1o, arrm[other])
+            vk = who(k2, mo)
+            vs = vec("ts", T.isl[:], T.zs[:].indirect(T.fi[:, 0:1]), 256.0, None, A.add)
+        if o == 1:
+            so = col(k2, T.q1o, vo, tu[other], tu[other ^ 1])
+    ids = [vec("copy", T.idf[:, 0:32], T.whow[:].indirect(T.isl[:, 0:2]), after=[vs, vf, vk]),
+           vec("copy", T.idf[:, 32:64], T.colw[:].indirect(T.isl[:, 0:2]), after=[sf, so])]
     for i in (0, 1):
+        wait("y", ids[i])
         inc("did", g.sync.dma_start(T.id[i:i + 1, :], T.idf[0:128:16, 32 * i:32 * i + 32]), 16)
 
-    wait("g", out1, outl, out2, outn, outm, arr1, *arrl.values(), arr2, arrn, arrm, *[(s, n) for s, n in cnt.items()])
+    wait("g", out1, outn, outk, out2, outm, arr1, arr2, *arrn.values(), *arrk.values(), *arrm.values(),
+         *[(s, n) for s, n in cnt.items()])

from concourse.bass import DstId, RemoteDMATransfer
from concourse.mybir import dt, AluOpType, ActivationFunctionType

K, O = 256, 4
H = 256
SCRATCH = {"ps": ("psum", [128, 4096], "float32")}


def _bufs(dtype, **widths):
    for name, n in widths.items():
        SCRATCH[name] = ("sbuf", [128, n], dtype)


_bufs("float8_e4m3fn_x4", cx=512, cu=128, cw=512, c1=512, c2=512)
_bufs("uint8", sx=512, su=128, sw=512, s1=512, s2=512)
_bufs("bfloat16", xb=2048, wb=2048, ub=16, up=512, neg=128, dm=128, fl=2048, cs=256, ce=512, f1=256, g1=128,
      val=64, win=800, wt=544, z=136, zs=136, rz=136, iot=256, rep=1024, colr=1024, whow=512,
      m0=6, m1=6, m2=6, m3=6, n0=16, n1=16, n2=16, n3=16)
_bufs("float32", sc4=4, nd=4, th=512, pl=4, vb=64, hc=1, fx=1, fy=1, fz=1, fw=1, k16=16, k256=16, kb=2, rv=256,
      h1=16, h2=16, h3=16, h4=16, k0=2, k1=2, k2=2, k3=2, sel=2, cp=1, t1=4, t2=4, t3=4,
      cc=1, colw=512, idf=64, yy=2048, ysb=1024)
_bufs("int32", ip=32, i3=32, i15=16, c16=16, c2i=16, ri=136, y17=1, a14=1, a112=1)
_bufs("uint16", u4=32, pou=4, fo=2, fi=2, isl=16, r32=16, lst=16, q1=16, q1o=16, q2=16)
SEMAPHORES = ["cv", "ca", "ct", "cp", "du", "dx0", "dx1", "dw", "dy0", "dy1", "did", "a1", "o1", "a2", "o2", "on", "ok", "om",
              "an0", "an1", "an2", "an3", "ak0", "ak1", "ak2", "ak3", "am0", "am1", "am2", "am3"]
STEP, TINY = 1.125 * 2.0 ** -24, 2.0 ** -124


def rank_program(g, core, T, topo):
    rank = T.rank_of(core)
    if rank is None:
        return
    A, F = AluOpType, ActivationFunctionType
    q = {"v": g.vector, "s": g.scalar, "t": g.tensor, "g": g, "y": g.sync}
    cnt, seen = {}, {}

    def inc(sem, ins, n=1):
        ins.then_inc(T.sem[sem], n)
        cnt[sem] = cnt.get(sem, 0) + n
        return (sem, cnt[sem])

    def wait(qn, *toks):
        best = {}
        for t in toks:
            best[t[0]] = max(best.get(t[0], 0), t[1])
        for sem, v in best.items():
            if seen.get((qn, sem), 0) < v:
                q[qn].wait_ge(T.sem[sem], v)
                seen[(qn, sem)] = v

    def vec(name, *args, after=()):
        wait("v", *after)
        calls = {"copy": g.vector.tensor_copy, "tt": g.vector.tensor_tensor, "ts": g.vector.tensor_scalar,
                 "set": g.vector.memset, "scan": g.vector.tensor_tensor_scan, "tr": g.vector.transpose,
                 "quant": g.vector.quantize_mx}
        return inc("cv", calls[name](*args))

    def act(out, in_, func, after=(), **kw):
        wait("s", *after)
        return inc("ca", g.scalar.activation(out, in_, func, **kw))

    def mm(out, a, sa, b, sb, after=()):
        wait("t", *after)
        return inc("ct", g.tensor.matmul_mx(out, a, sa, b, sb, True, True))

    mate, other = rank ^ 1, rank ^ 2
    lower = rank < mate
    a0 = 0 if lower else H
    b0 = H - a0
    f2 = 0 if rank < other else 1
    k2 = 1 - f2
    blk = 0 if lower else 1

    du = inc("du", g.scalar.dma_start(T.ub[:, 0:4], T.u[:, 0:4]), 16)
    dx = [inc("dx%d" % h, g.sync.dma_start(T.xb[:, 1024 * h:1024 * h + 1024], T.x[:, 1024 * h:1024 * h + 1024]), 16)
          for h in (0, 1)]
    dw = inc("dw", g.sync.dma_start(T.wb[:], T.w[:]), 16)

    vneg = vec("set", T.neg[:], -1.0)
    f = {"allow_small_or_imprecise_dtypes": True}
    pip = inc("cp", g.iota(T.ip[:], [[0, 32]], 0, 1))
    wait("g", vneg)
    pdm = inc("cp", g.affine_select(T.dm[:], T.neg[:], [[-1, 128]], A.is_gt if lower else A.is_ge, 0.0, 0, 1))
    pri = inc("cp", g.iota(T.ri[:], [[0, 17], [1, 8]], 0, 0))
    pvb = inc("cp", g.iota(T.vb[:], [[128, 4], [1, 16]], 0, 0, **f))
    pc16 = inc("cp", g.iota(T.c16[:], [[16, 16]], 0, 0))
    pc2 = inc("cp", g.iota(T.c2i[:], [[1, 8], [0, 2]], 0, 0))
    piot = inc("cp", g.iota(T.iot[:], [[1, 256]], -256, 0, **f))
    pkb = inc("cp", g.iota(T.kb[:], [[128 if lower else -128, 2]], -256 if lower else -1, 1 if lower else -1, **f))
    v = vec("ts", T.i3[:], T.ip[:], 3, None, A.bitwise_and, after=[pip])
    vu4 = vec("copy", T.u4[:], T.i3[:], after=[v])
    v15 = vec("ts", T.i15[:], T.ip[:, 0:16], 15, None, A.bitwise_and)
    for out, bits in ((T.y17, 17), (T.a14, 14), (T.a112, 112)):
        va = vec("ts", out[:], T.ip[:, 0:1], bits, None, A.bitwise_and)
    w0 = 32 if lower else 32 + H
    vwin = vec("set", T.win[:, w0 - 16:w0 + 272], 0.0)
    s = act(T.up[:, 256:512], T.ub[:, 0:4].indirect(T.u4[:, 16:32]), F.Copy, after=[du, vu4])
    v = vec("copy", T.up[:, 0:256], T.ub[:, 0:4].indirect(T.u4[:, 0:16]), after=[du, vu4])
    vqu = vec("quant", T.cu[:], T.su[:], T.up[:], after=[v, s])
    vec("tt", T.hc[:], T.ip[:, 0:1], T.i15[:, 0:1], A.subtract, after=[v15])
    vec("ts", T.fx[:], T.y17[:], 1, 72.0, A.is_equal, A.mult, after=[va])
    vec("ts", T.fy[:], T.y17[:], 16, 64.0, A.is_equal, A.mult)
    vec("ts", T.fz[:], T.a14[:], 4.0, 7.0, A.mult, A.add)
    vf = vec("ts", T.fw[:], T.a112[:], 0.5, 7.0, A.mult, A.add)

    def constants():
        vec("ts", T.fo[:, 0:1], T.fx[:], T.fy[:], T.fz[:], A.add, A.add, after=[vf])
        vfo = vec("ts", T.fi[:, 0:1], T.fx[:], T.fy[:], T.fw[:], A.add, A.add)
        vrz = vec("ts", T.rz[:], T.ri[:], 0, None, A.is_gt, after=[pri])
        vval = vec("ts", T.val[:], T.vb[:], T.hc[:], -256.0, A.add, A.add, after=[pvb, vf])
        return vfo, vrz, vval

    def score_half(h, toks, row_first):
        def row():
            return mm(T.ps[:, 512 * h:512 * h + H], T.cu[:], T.su[:], T.cx[:, H * h:H * h + H], T.sx[:, H * h:H * h + H])

        wait("t", *toks)
        r = row() if row_first else None
        for t in (2 * h, 2 * h + 1):
            x = mm(T.ps[:, 512 * (2 + t):512 * (2 + t) + 128], T.cx[:, 128 * t:128 * t + 128],
                   T.sx[:, 128 * t:128 * t + 128], T.cu[:], T.su[:])
        return x, r or row()

    def column(h, tx):
        return act(T.sc4[:, 2 * h:2 * h + 2], T.ps[:, 512 * (2 + 2 * h):512 * (4 + 2 * h):512], F.Copy, after=[tx])

    def inside(h, sc):
        n = act(T.nd[:, 2 * h:2 * h + 2], T.ps[:, 512 * (2 + 2 * h):512 * (4 + 2 * h):512], F.Abs, scale=STEP, bias=TINY)
        return [act(T.th[:, 128 * t:128 * t + 128], T.dm[:], F.Identity, after=[sc, n, pdm],
                    scale=T.nd[:, t:t + 1], bias=T.sc4[:, t:t + 1]) for t in (2 * h, 2 * h + 1)]

    def plain(t, j0, j1, at, toks=()):
        p = 512 * (j0 // H) + j0 % H
        if j1 <= 128 * t:
            op = A.is_ge if lower else A.is_lt
        else:
            op = A.is_gt if lower else A.is_le
        return vec("ts", T.fl[:, 512 * t + at:512 * t + at + j1 - j0], T.ps[:, p:p + j1 - j0], T.sc4[:, t:t + 1], None,
                   op, after=toks)

    def diag(t, at, tok):
        p = 512 * (t // 2) + 128 * (t % 2)
        return vec("tt", T.fl[:, 512 * t + at:512 * t + at + 128], T.ps[:, p:p + 128], T.th[:, 128 * t:128 * t + 128],
                   A.is_gt if lower else A.is_le, after=[tok])

    def total(t, i0, i1, tok):
        fl = T.fl[:, 512 * t + i0:512 * t + i1]
        return act(fl, fl, F.Copy, after=[tok], accum_out=T.pl[:, t:t + 1])

    def halves(z, cs, j, tok):
        return vec("scan", cs[:, j:j + 128], T.fl[:, z:z + 128], T.fl[:, z + 128:z + 256], 0.0, A.add, A.add, after=[tok])

    def row_sum(t, tok):
        z, j = 512 * t, 256 * (t // 2)
        return vec("scan", T.ce[:, j:j + 256], T.fl[:, z:z + 256], T.fl[:, z + 256:z + 512], -256.0, A.add, A.add, after=[tok])

    def cross(t, h, at, toks=()):
        return plain(t, H * h, H * h + H, at, toks)

    def places(f, k, sc, trk):
        a = cross(2 * f, k, H, [trk])
        b = cross(2 * f + 1, k, H)
        th = inside(k, sc)
        s0 = total(2 * f, 0, 512, a)
        cross(2 * k, f, 0, [sc])
        row_sum(2 * f + 1, b)
        plain(2 * k, H * k + 128, H * k + 256, H + 128)
        s1 = total(2 * k, 0, 512, diag(2 * k, H, th[0]))
        t = 2 * k + 1
        cross(t, f, 0)
        plain(t, H * k, H * k + 128, H)
        e = row_sum(t, diag(t, H + 128, th[1]))
        vec("ts", T.pou[:, 1:4:2], T.ce[:, 255:512:256], 256.0, None, A.add, after=[e])
        return vec("copy", T.pou[:, 0:4:2], T.pl[:, 0:4:2], after=[s0, s1])

    def to_list(e, out, w0, w1, n):
        e = vec("copy", T.win[:, 32:w1].indirect(T.pou[:]), T.val[:], after=[e, vval, vwin])
        vec("tr", T.wt[:, 0:256], T.win[:, w0:w0 + 256], after=[e])
        e = vec("tr", T.wt[:, 256:544], T.win[:, w0 - 16:w0 + 272])
        runs = [(0, 128, 0, 0), (0, 64, 2, 1), (2, 64, 0, 1), *[(d, 32, d ^ 1, 2) for d in range(4)],
                *[(d, 32, d ^ 3, 3) for d in range(4)]]
        toks = []
        for i, (d, m, src, j) in enumerate(runs):
            ab = T.z[32 * d:32 * d + m, j:136:4], T.wt[32 * src:32 * src + m, 0:544:16]
            toks.append(vec("copy", *ab, after=[e]) if i < 11 - n else act(*ab, F.Copy, after=[e]))
        e = vec("scan", T.zs[:], T.rz[:], T.z[:], 0.0, A.mult, A.add, after=[*toks, vrz])
        return e, vec("ts", out[:], T.zs[:].indirect(T.fo[:, 0:1]), 256.0, None, A.add, after=[e, vfo])

    def pick(c_to, s_to, j, c, s, i0, i1, off, *toks):
        v = vec("copy", c_to[:, j:j + K].bitcast(dt.uint32), c[:, i0:i1].bitcast(dt.uint32).indirect(off[:]), after=toks)
        return v, act(s_to[:, j:j + K], s[:, i0:i1].indirect(off[:]), F.Copy, after=toks)

    vq = vec("quant", T.cx[:, 0:H], T.sx[:, 0:H], T.xb[:, 0:1024], after=[dx[0]])
    tx, tr0 = score_half(0, [vqu, vq], False)
    sc0 = column(0, tx)
    th0 = inside(0, sc0)
    vfo, vrz, vval = constants()
    vq = vec("quant", T.cx[:, H:2 * H], T.sx[:, H:2 * H], T.xb[:, 1024:2048], after=[dx[1]])
    plain(0, 128, 256, 128, [sc0, tr0])
    plain(1, 0, 128, 0)
    diag(0, 0, th0[0])
    diag(1, 128, th0[1])
    tx, tr1 = score_half(1, [vq], True)
    zl, ql = to_list(places(0, 1, column(1, tx), tr1), T.lst, w0, 544, 5)

    def send(c, s, j, to, arr, out, pk):
        rid, pid, _ = topo.addr(T.cores[to])
        m, n = topo.mask(core, T.cores[to]), len(topo.engines(core, T.cores[to]))
        wait("g", pk[0])
        cc = c[:, j:j + K].bitcast(dt.uint8)
        g.remote_dma(cc, cc, T.sem[arr], T.sem[out], pid, rid, m)
        wait("g", pk[1])
        g.remote_dma(s[:, j:j + K], s[:, j:j + K], T.sem[arr], T.sem[out], pid, rid, m)
        return (arr, 2 * n), (out, 2 * n)

    def tell(what, n, *toks):
        tr, arr = [], {}
        for i, r in enumerate((mate, other, other ^ 1)):
            rid, pid, _ = topo.addr(T.cores[r])
            eng = topo.engines(core, T.cores[r])[4 * i:4 * i + 4]
            me = T["%s%d" % (what, rank)][:, 0:n]
            tr.append(RemoteDMATransfer(dst_ids=[DstId(rid=rid, pnc=pid)], dma_engine_mask=sum(1 << e for e in eng),
                                        remote_sem=T.sem["a%s%d" % (what, rank)], src=me, dst=me))
            arr[r] = ("a%s%d" % (what, r), 4)
        wait("g", *toks)
        g.remote_dma_fused(tr, local_sem=T.sem["o" + what])
        return arr, ("o" + what, 12)

    snum = act(T["n%d" % rank][:, 0:8], T.zs[:, 7:64:8], F.Copy, after=[zl])
    arrn, outn = tell("n", 8, snum)
    p1 = pick(T.c1, T.s1, a0, T.cx, T.sx, 0, 512, T.lst, ql)
    arr1, out1 = send(T.c1, T.s1, a0, mate, "a1", "o1", p1)
    wait("t", *p1)
    for t in (0, 1):
        tx = mm(T.ps[:, 512 * (2 + t):512 * (2 + t) + 128], T.c1[:, a0 + 128 * t:a0 + 128 * t + 128],
                T.s1[:, a0 + 128 * t:a0 + 128 * t + 128], T.cu[:], T.su[:])
    sk = act(T["k%d" % rank][:, 0:2], T.ps[:, 1024:2048:512], F.Copy, after=[tx])
    arrk, outk = tell("k", 2, sk)

    vr32 = vec("copy", T.r32[:], T.c2i[:], after=[pc2])
    vk16 = vec("tt", T.k16[:], T.i15[:], T.c16[:], A.add, after=[pc16])
    vec("ts", T.k256[:], T.k16[:], -256.0, None, A.add, after=[vk16])
    vm = vec("set", T["m%d" % rank][:], 0.0)
    vw = vec("quant", T.cw[:], T.sw[:], T.wb[:], after=[dw])
    vwin = vec("set", T.win[:, 16:304], 0.0)

    def replicated(r):
        return act(T.rep[:, 256 * r:256 * r + 256], T["n%d" % r][:, 0:8].indirect(T.r32[:]), F.Copy,
                   after=[vr32, snum if r == rank else arrn[r]])

    def turned(r, tok):
        return vec("tr", T.colr[:, 256 * r:256 * r + 256], T.rep[:, 256 * r:256 * r + 256], after=[tok])

    rp = {rank: replicated(rank)}
    t = mm(T.ps[:, 0:256], T.cu[:], T.su[:], T.c1[:, a0:a0 + H], T.s1[:, a0:a0 + H])
    srv = act(T.rv[:], T.ps[:, 0:256], F.Copy, after=[t])
    for r in (mate, other):
        rp[r] = replicated(r)
    tu = {r: turned(r, rp[r]) for r in (rank, mate)}

    def kk(r, t, n=1):
        return T["k%d" % r][:, t:t + n]

    vcp = vec("tt", T.cp[:], kk(other, blk), kk(other ^ 1, blk), A.max, after=[arrk[other], arrk[other ^ 1]])
    vsel = vec("tt", T.sel[:], kk(rank, 0, 2), kk(mate, 0, 2), A.is_ge if lower else A.is_gt, after=[arrk[mate], sk])

    def sides(at, row, *toks):
        return act(T.fl[:, at:at + H], row, F.Sign, scale=-1.0, bias=T.cp[:], after=[vcp, *toks])

    sides(0, T.rv[:], srv)

    row = [mm(T.ps[:, b:b + H], T.cu[:], T.su[:], T.c1[:, b0:b0 + H], T.s1[:, b0:b0 + H], after=[arr1, sk]) for b in (512, 1024)]
    theirs = T.ps[:, 512:768]
    rows = (T.rv[:], theirs) if lower else (theirs, T.rv[:])
    v = vec("tt", T.f1[:], rows[0], rows[1], A.is_ge, after=[row[0], srv])
    mine = T.g1[:, 127:128]
    vm1 = vec("scan", T.g1[:], T.f1[:, 0:128], T.f1[:, 128:256], -256.0, A.add, A.add, after=[v])

    def choice(m, h1, h2, out, *toks):
        v = vec("ts", h1[:], T.k256[:], m, 256.0, A.is_ge, A.mult, after=toks)
        v = vec("tt", h2[:], T.k16[:], h1[:], A.add, after=[v])
        return vec("copy", out[:], h2[:], after=[v])

    vc = choice(mine, T.h1, T.h2, T.q1, vm1)
    ss = sides(H, T.ps[:, 1024:1280], row[1])
    p2 = pick(T.c2, T.s2, H * f2, T.c1, T.s1, 0, 512, T.q1, vc, arr1, *p1)

    arr2, out2 = send(T.c2, T.s2, H * f2, other, "a2", "o2", p2)

    msg = T["m%d" % rank]
    sc = act(T.fl[:, 512:1024], T.fl[:, 0:512], F.Relu, scale=1.0 if f2 == 0 else -1.0, accum_out=T.cc[:], after=[ss])
    smine = act(msg[:, 4:5], mine, F.Copy, after=[vm1, vm])
    c = [vec("ts", T.fl[:, 1024 + H * i:1280 + H * i], theirs, kk(rank, i), None, A.is_gt if lower else A.is_ge)
         for i in (0, 1)]
    c = [halves(1024 + H * i, T.cs, 128 * i, c[i]) for i in (0, 1)]
    for i in (0, 1):
        at = 2 * f2 + i
        vec("ts", msg[:, at:at + 1], T.cs[:, 128 * i + 127:128 * i + 128], T.kb[:, i:i + 1], T.sel[:, i:i + 1],
            A.add, A.mult, after=[c[i], pkb, vsel, vm])
    at, sign = 2 * k2 + blk, -1.0 if f2 == 0 else 1.0
    vmsg = vec("ts", msg[:, at:at + 1], T.cc[:], sign, -256.0 * sign, A.mult, A.add, after=[sc])
    arrm, outm = tell("m", 6, vmsg, smine)

    def products(h, banks, toks):
        return [mm(T.ps[:, 512 * b:512 * b + H], T.cw[:, 128 * o:128 * o + 128], T.sw[:, 128 * o:128 * o + 128],
                   T.c2[:, H * h:H * h + H], T.s2[:, H * h:H * h + H], after=toks) for o, b in enumerate(banks)]

    def result(h, o, b):
        return T.yy[:, 512 * o + H * h:512 * o + H * h + H], T.ps[:, 512 * b:512 * b + H]

    def col(h, lists, *toks):
        return act(T.colw[:, H * h:H * h + H], T.colr[:, 512 * h:512 * h + 512].indirect(lists[:]), F.Identity, bias=256.0,
                   after=toks)

    def who(h, m, *toks):
        return vec("ts", T.whow[:, H * h:H * h + H], T.iot[:], m, 2.0 * h, A.is_ge, A.add, after=[piot, *toks])

    bf, bk = [4, 5, 6, 7], [2, 3, 0, 1]
    typ = products(f2, bf, [vw, *p2])
    vf = who(f2, mine)
    tu[other] = turned(other, rp[other])
    done = [act(*result(f2, o, bf[o]), F.Copy, after=[typ[o]]) for o in (0, 1)]
    rp[other ^ 1] = replicated(other ^ 1)
    done += [vec("copy", *result(f2, o, bf[o]), after=[typ[o]]) for o in (2, 3)]
    tu[other ^ 1] = turned(other ^ 1, rp[other ^ 1])
    sf = col(f2, T.q1, vc, tu[rank], tu[mate])
    tyq = products(k2, bk, [arr2, sk, srv, vmsg, ss])

    def m4(r):
        return T["m%d" % r][:, 0:4]

    def results(*os):
        return [act(*result(k2, o, bk[o]), F.Copy, after=[tyq[o]]) for o in os]

    there = results(0, 1)
    v = vec("tt", T.t1[:], m4(rank), m4(mate), A.add, after=[vmsg, arrm[mate]])
    v = vec("tt", T.t2[:], T.t1[:], m4(other), A.add, after=[v, arrm[other]])
    v = vec("tt", T.t3[:], T.t2[:], m4(other ^ 1), A.add, after=[v, arrm[other ^ 1]])
    v = vec("ts", T.pou[:], T.t3[:], 512.0, None, A.add, after=[v])
    v2 = to_list(v, T.q2, 32, 800, 3)[1]
    there += results(2, 3)

    mo = T["m%d" % other][:, 4:5]
    for o in range(O):
        src, out = T.yy[:, 512 * o:512 * o + 512].indirect(T.q2[:]), T.ysb[:, K * o:K * o + K]
        toks = [v2, done[o], there[o]]
        tok = vec("copy", out, src, after=toks) if o % 2 == 0 else act(out, src, F.Copy, after=toks)
        y = "s" if o == 3 else "y"
        wait(y, tok)
        inc("dy%d" % (o == 3), q[y].dma_start(T.y[:, K * o:K * o + K], out), 16)
        if o == 0:
            vo = choice(mo, T.h3, T.h4, T.q1o, arrm[other])
            vk = who(k2, mo)
            vs = vec("ts", T.isl[:], T.zs[:].indirect(T.fi[:, 0:1]), 256.0, None, A.add)
        if o == 1:
            so = col(k2, T.q1o, vo, tu[other], tu[other ^ 1])
    ids = [vec("copy", T.idf[:, 0:32], T.whow[:].indirect(T.isl[:, 0:2]), after=[vs, vf, vk]),
           vec("copy", T.idf[:, 32:64], T.colw[:].indirect(T.isl[:, 0:2]), after=[sf, so])]
    for i in (0, 1):
        wait("y", ids[i])
        inc("did", g.sync.dma_start(T.id[i:i + 1, :], T.idf[0:128:16, 32 * i:32 * i + 32]), 16)

    wait("g", out1, outn, outk, out2, outm, arr1, arr2, *arrn.values(), *arrk.values(), *arrm.values(),
         *[(s, n) for s, n in cnt.items()])
